import numpy as np
import ml_dtypes


def mxq(x, axis, fmt="e4m3"):
    dtype, down = {"e4m3": (ml_dtypes.float8_e4m3fn, 7), "e5m2": (ml_dtypes.float8_e5m2, 14)}[fmt]
    v = np.moveaxis(np.asarray(x, np.float32).astype(ml_dtypes.bfloat16).astype(np.float64), axis, -1)
    blocks = v.reshape(v.shape[:-1] + (-1, 32))
    amax = np.abs(blocks).max(-1, keepdims=True)
    byte = np.maximum(np.where(amax > 0, np.frexp(amax)[1] - 1 + 127, 0) - down, 1)
    scale = np.exp2(byte - 127.0)
    codes = (blocks / scale).astype(np.float32).astype(dtype).astype(np.float64)
    return np.moveaxis((codes * scale).reshape(v.shape), -1, axis)


WIDE = False


def mx_kscale(k):
    if not WIDE:
        return np.ones(k)
    levels = np.array([10, -10, 5, -5, 0])
    if k % 512:
        return np.exp2(np.random.permutation(np.resize(levels, k // 32))).repeat(32)
    a = np.empty((k // 512, 16))
    for p in range(k // 512):
        a[p, :8] = np.random.permutation(np.resize(levels, 8))
        for g in range(8):
            far = levels[np.abs(levels - a[p, g]) >= 10]
            a[p, g + 8] = far[np.random.randint(len(far))]
    return np.exp2(a.ravel()).repeat(32)


BF16 = ml_dtypes.bfloat16


def bf(x):
    return np.asarray(x, np.float32).astype(BF16)


def f64(x):
    return np.asarray(x).astype(np.float64)


T, D, F = 2048, 1024, 1024


def erf(u):
    c = np.clip(u, -6.0, 6.0)
    q = 2.0 * c * c
    term = np.array(c)
    total = np.array(c)
    for n in range(1, 151):
        term *= q / (2 * n + 1)
        total += term
    return np.where(np.abs(u) > 6.0, np.sign(u), 2.0 / np.sqrt(np.pi) * np.exp(-c * c) * total)


def gelu_erf_grad(a):
    cdf = 0.5 * (1.0 + erf(a / np.sqrt(2.0)))
    pdf_term = a * np.exp(-np.square(a) / 2.0) / np.sqrt(2.0 * np.pi)
    return cdf + pdf_term


def frobenius(z):
    return np.sqrt(np.sum(np.square(z), axis=(0, 1)))


def draw0():
    s, t = mx_kscale(D), mx_kscale(T)
    return {
        "x": bf(np.random.standard_normal((T, D)) / t[:, None]),
        "a": bf(np.random.standard_normal((T, F))),
        "dy": bf(np.random.standard_normal((T, D)) * s[None, :] * t[:, None]),
        "w2": bf(np.random.standard_normal((F, D)) / np.sqrt(D) / s[None, :]),
        "w1": bf(np.random.standard_normal((D, F))),
        "m": bf(np.random.standard_normal((D, F)) * 0.3),
        "v": bf(np.random.uniform(0.2, 1.0, (D, F))),
    }


def core(x, a, dy, w2, w1, m, v):
    x, a, dy, w2, w1, m, v = f64(x), f64(a), f64(dy), f64(w2), f64(w1), f64(m), f64(v)
    tokens = x.shape[0]
    dh = mxq(dy, 1, "e4m3") @ mxq(w2, 1, "e4m3").T
    da = dh * gelu_erf_grad(a)
    g = (mxq(x, 0, "e4m3").T @ mxq(da, 0, "e4m3")) / np.sqrt(tokens)
    m_new = 0.6 * m + 0.4 * g
    v_new = 0.6 * v + 0.4 * np.square(g)
    r = m_new / np.sqrt(v_new) + 0.1 * w1
    trust = frobenius(w1) / frobenius(r)
    return w1 - 0.5 * trust * r


def e4m3fn_bytes(y):
    return np.clip(np.asarray(y, np.float64), -448.0, 448.0).astype(np.float32).astype(ml_dtypes.float8_e4m3fn).view(np.uint8)


def e4m3fn_values(b):
    return np.asarray(b, np.uint8).view(ml_dtypes.float8_e4m3fn).astype(np.float64)


def setup_inputs():
    d = draw0()
    x0 = np.asarray(d['x']).astype(np.float64)
    s = (np.max(np.abs(x0), axis=(1,), keepdims=True) / 448.0).astype(np.float32)
    out = {}
    for k, v in d.items():
        if k == 'x':
            out['x_bytes'] = e4m3fn_bytes(x0 / s.astype(np.float64))
            out['x_scale'] = s
        else:
            out[k] = v
    return out


def reference(x_bytes, x_scale, a, dy, w2, w1, m, v):
    return core(e4m3fn_values(x_bytes) * x_scale.astype(np.float64), a, dy, w2, w1, m, v)

@@ -1,0 +1,669 @@
+from contextlib import ExitStack
+import math
+import concourse.mybir as mybir
+from concourse.masks import make_identity
+
+T, D, F = 2048, 1024, 1024
+F32 = mybir.dt.float32
+BF16 = mybir.dt.bfloat16
+U32 = mybir.dt.uint32
+U8 = mybir.dt.uint8
+FP8 = mybir.dt.float8_e4m3fn
+X4 = mybir.dt.float8_e4m3fn_x4
+ACT = mybir.ActivationFunctionType
+ALU = mybir.AluOpType
+AX = mybir.AxisListType
+P = 128
+NG = 4
+NU = 8
+FLOPS = 2 * 2 * T * D * F + 40 * T * F
+DELTA = 2.0 ** -60
+INV_SQRT_2PI = 1.0 / math.sqrt(2.0 * math.pi)
+
+
+def tile_lambmlpbackwardstep_kernel(tc, x_bytes, x_scale, a, dy, w2, w1, m, v, out):
+    nc = tc.nc
+    with ExitStack() as ctx:
+        TB, DB = 2, 3
+        NBIG, NSMALL = 13, 5
+        SLOTS = {
+            "big": [8192 * s for s in range(NBIG)],
+            "turn": [8192 * (NBIG + s) for s in range(4)],
+            "small": [8192 * (NBIG + 4) + 4096 * s for s in range(NSMALL)],
+        }
+        OFF = {}
+        WF, NB, A_USE, MV_USE = {}, [], [], []
+        keep = ctx.enter_context(tc.tile_pool(name="keep", bufs=1))
+        mem = ctx.enter_context(tc.tile_pool(name="mem", bufs=1))
+        ps = ctx.enter_context(tc.psum_pool(name="ps", bufs=2))
+        ctx.enter_context(tc.manual_schedule())
+
+        ident = keep.tile([P, P], F32, name="ident")
+        ones = keep.tile([P, P], F32, name="ones")
+        xs = keep.tile([P, NG, 4], F32, name="xs")
+        x_codes = keep.tile([P, NG, D], U32, name="x_codes", align_bytes=64)
+        x_planes = keep.tile([P, NG, D], U8, name="x_planes", align_bytes=64)
+        dy_codes = keep.tile([P, 2, T], U32, name="dy_codes", align_bytes=64)
+        dy_planes = keep.tile([P, 2, T], U8, name="dy_planes", align_bytes=64)
+        w2_codes = keep.tile([P, 2, F], U32, name="w2_codes", align_bytes=64)
+        w2_planes = keep.tile([P, 2, F], U8, name="w2_planes", align_bytes=64)
+        w1_sb = keep.tile([P, 8, F], BF16, name="w1_sb")
+        stat = keep.tile([P, 32], F32, name="stat")
+        wtot = keep.tile([P, 8], F32, name="wtot")
+
+        A, XB, RAW, MV = {}, {}, {}, {}
+        R, E, G, GRP, XW, XI, DQ, DC, DPL, S2, SQ, S1 = ({} for n in range(12))
+
+        def take(kind, name, shape, dtype):
+            OFF[name] = (kind, SLOTS[kind].pop(0))
+            return mem.tile(shape, dtype, name=name, bufs=1, offset=OFF[name][1], align_bytes=64)
+
+        def give(name):
+            kind, off = OFF.pop(name)
+            SLOTS[kind].append(off)
+
+        def load_a(i, g=None):
+            if i not in A:
+                A[i] = take("big", "a%d" % i, [P, 16, 256], BF16)
+            src = a.rearrange("(g p t) f -> p g t f", g=NG, t=4)
+            gs = range(NG) if g is None else [g]
+            for q in gs:
+                nc.sync.dma_start(out=A[i][:, 4 * q:4 * q + 4, :], in_=src[:, q, :, 256 * i:256 * (i + 1)])
+
+        def load_x(g):
+            XB[g] = take("small", "xb%d" % g, [P, 4, D], U8)
+            nc.sync.dma_start(out=XB[g][:], in_=x_bytes.rearrange("(g p t) d -> g p t d", g=NG, t=4)[g])
+
+        def load_raw(kind, q):
+            t = take("turn", "raw%s%d" % (kind, q), [P, 4, D], BF16)
+            RAW[kind, q] = t
+            if kind == "dy":
+                src = dy.rearrange("(g p t) k -> g p t k", g=NG, t=4)[q]
+            else:
+                src = w2.rearrange("(h b p) k -> h p b k", h=2, b=4)[q]
+            nc.sync.dma_start(out=t[:], in_=src)
+
+        def load_mv(i):
+            t = take("big", "mv%d" % i, [P, 16, 256], BF16)
+            for n, (k, src) in enumerate((("m", m), ("v", v))):
+                MV[k, i] = t[:, 8 * n:8 * n + 8, :]
+                nc.sync.dma_start(out=MV[k, i], in_=src.rearrange("(i p) f -> p i f", p=P)[:, :, 256 * i:256 * (i + 1)])
+
+        def load_w1():
+            nc.sync.dma_start(out=w1_sb[:], in_=w1.rearrange("(i p) f -> p i f", p=P))
+
+        def done_a(j):
+            A_USE.append(j // 2)
+            if A_USE.count(j // 2) == 4:
+                give("a%d" % (j // 2))
+
+        def a_unit(j):
+            return A[j // 2][:, :, 128 * (j % 2):128 * (j % 2) + 128]
+
+        def z(j, first, gs=None):
+            d = E if first else R
+            if j not in d:
+                d[j] = take("big", ("e%d" if first else "r%d") % j, [P, 16, P], F32)
+            sl = slice(0, 16) if gs is None else slice(4 * gs[0], 4 * gs[-1] + 4)
+            nc.scalar.activation(out=d[j][:, sl, :], in_=a_unit(j)[:, sl, :], func=ACT.Square)
+
+        def rr_(j, first):
+            if first:
+                R[j] = take("big", "r%d" % j, [P, 16, P], F32)
+                src = E[j]
+            else:
+                src = R[j]
+            nc.scalar.activation(out=R[j][:], in_=src[:], func=ACT.Abs_reciprocal_sqrt, bias=DELTA * DELTA)
+
+        def e(j, first):
+            if first:
+                src = E[j]
+            else:
+                E[j] = take("big", "e%d" % j, [P, 16, P], F32)
+                src = R[j]
+            nc.scalar.activation(out=E[j][:], in_=src[:], func=ACT.Exp, scale=-0.5)
+
+        def gl(j):
+            G[j] = take("big", "g%d" % j, [P, 16, P], F32)
+            nc.scalar.activation(out=G[j][:], in_=a_unit(j), func=ACT.Gelu, bias=DELTA)
+            done_a(j)
+
+        def ab(j):
+            nc.scalar.activation(out=G[j][:], in_=G[j][:], func=ACT.Abs)
+
+        BK = {}
+
+        def tp(kind, q, c, b):
+            bank = ps.tile([P, 2, 2, P], F32, name="tp", bufs=TB)
+            BK[kind, q, c, b] = bank
+            for k in range(2):
+                w = RAW[kind, q][:, 2 * b + k, :].bitcast(F32)
+                for u in range(2):
+                    nc.tensor.transpose(out=bank[:, k, u, :], in_=w[:, 256 * c + u:256 * (c + 1):2], identity=ident[:])
+
+        def tcopy(kind, q, c, b, eng):
+            if b == 0:
+                GRP[kind, q, c] = take("small", "grp%s%d%d" % (kind, q, c), [P, 2048], BF16)
+            dst = GRP[kind, q, c][:].bitcast(F32)[:, 512 * b:512 * b + 512].rearrange("p (j r u) -> p j r u", j=2, u=2)
+            src = BK[kind, q, c, b][:].rearrange("p j u r -> p j r u")
+            if eng == "S":
+                nc.scalar.copy(out=dst, in_=src)
+            else:
+                nc.vector.tensor_copy(out=dst, in_=src)
+
+        def tquant(kind, q, c):
+            codes, planes = (dy_codes, dy_planes) if kind == "dy" else (w2_codes, w2_planes)
+            sl = slice(512 * q, 512 * q + 512)
+            nc.vector.quantize_mx(out=codes[:, c, sl].bitcast(X4), scales=planes[:, c, sl], in_=GRP[kind, q, c][:])
+            give("grp%s%d%d" % (kind, q, c))
+            if c == 1:
+                give("raw%s%d" % (kind, q))
+
+        def xw(g, ts=(0, 1, 2, 3), eng="V"):
+            if g not in XW:
+                XW[g] = take("big", "xw%d" % g, [P, 4, D], BF16)
+            for t in ts:
+                src = XB[g][:, t, :].bitcast(FP8)
+                if eng == "V":
+                    nc.vector.tensor_scalar(out=XW[g][:, t, :], in0=src, scalar1=xs[:, g, t:t + 1], scalar2=None, op0=ALU.mult)
+                else:
+                    nc.scalar.activation(out=XW[g][:, t, :], in_=src, func=ACT.Copy, scale=xs[:, g, t:t + 1])
+                if t == 3:
+                    give("xb%d" % g)
+
+        def xi(g, h):
+            if h == 0:
+                XI[g] = take("big", "xi%d" % g, [P, 4096], BF16)
+            nc.vector.tensor_copy(out=XI[g][:, 2048 * h:2048 * h + 2048].rearrange("p (n t) -> p n t", t=4), in_=XW[g][:, :, 512 * h:512 * h + 512].rearrange("p t n -> p n t"))
+            if h == 1:
+                give("xw%d" % g)
+
+        def xq(g):
+            nc.vector.quantize_mx(out=x_codes[:, g, :].bitcast(X4), scales=x_planes[:, g, :], in_=XI[g][:])
+            give("xi%d" % g)
+
+        def v1(j):
+            nc.vector.tensor_tensor(out=G[j][:], in0=G[j][:], in1=R[j][:], op=ALU.mult)
+            give("r%d" % j)
+
+        def v2(j):
+            nc.vector.scalar_tensor_tensor(out=E[j][:], in0=a_unit(j), scalar=INV_SQRT_2PI, in1=E[j][:], op0=ALU.mult, op1=ALU.mult)
+            done_a(j)
+
+        def v3(j):
+            nc.vector.tensor_tensor(out=G[j][:], in0=G[j][:], in1=E[j][:], op=ALU.add)
+            give("e%d" % j)
+
+        def s1(j, g):
+            bank = ps.tile([P, 4, P], F32, name="dh", bufs=DB)
+            S1[j, g] = bank
+            for t in range(4):
+                for c in range(2):
+                    col = 512 * g + 128 * t
+                    nc.tensor.matmul_mx(
+                        out=bank[:, t, :], lhsT=dy_codes[:, c, col:col + 128].bitcast(X4), lhsT_scale=dy_planes[:, c, col:col + 128],
+                        rhs=w2_codes[:, c, 128 * j:128 * j + 128].bitcast(X4), rhs_scale=w2_planes[:, c, 128 * j:128 * j + 128],
+                        start=(c == 0), stop=(c == 1))
+
+        def v4(j, g):
+            if g == 0:
+                DQ[j] = take("small", "daq%d" % j, [P, 2048], BF16)
+            nc.vector.tensor_tensor(
+                out=DQ[j][:, 512 * g:512 * g + 512].rearrange("p (n t) -> p n t", t=4),
+                in0=S1[j, g][:].rearrange("p t n -> p n t"), in1=G[j][:, 4 * g:4 * g + 4, :].rearrange("p t n -> p n t"), op=ALU.mult)
+            if g == 3:
+                give("g%d" % j)
+
+        def q(j):
+            DC[j] = keep.tile([P, 512], U32, name="dac", bufs=2, align_bytes=64)
+            DPL[j] = keep.tile([P, 512], U8, name="dap", bufs=2, align_bytes=64)
+            nc.vector.quantize_mx(out=DC[j][:].bitcast(X4), scales=DPL[j][:], in_=DQ[j][:])
+            give("daq%d" % j)
+
+        def s2(j, hb):
+            bank = ps.tile([P, 4, P], F32, name="gp", bufs=2)
+            S2[j, hb] = bank
+            for k in range(4):
+                i = 4 * hb + k
+                for g in range(NG):
+                    nc.tensor.matmul_mx(
+                        out=bank[:, k, :], lhsT=x_codes[:, g, 128 * i:128 * i + 128].bitcast(X4), lhsT_scale=x_planes[:, g, 128 * i:128 * i + 128],
+                        rhs=DC[j][:, 128 * g:128 * g + 128].bitcast(X4), rhs_scale=DPL[j][:, 128 * g:128 * g + 128],
+                        start=(g == 0), stop=(g == NG - 1))
+
+        def fc(j):
+            return slice(128 * (j % 2), 128 * (j % 2) + 128)
+
+        def sq(j, hb):
+            if hb == 0:
+                SQ[j] = take("small", "sq%d" % j, [P, 8, P], F32)
+            nc.scalar.activation(out=SQ[j][:, 4 * hb:4 * hb + 4, :], in_=S2[j, hb][:], func=ACT.Square, scale=math.sqrt(0.4 / 0.6 / T))
+
+        def p_(j, hb):
+            nc.vector.scalar_tensor_tensor(
+                out=r_sb[:, 4 * hb:4 * hb + 4, 128 * j:128 * j + 128], in0=MV["m", j // 2][:, 4 * hb:4 * hb + 4, fc(j)], scalar=1.5 * math.sqrt(T),
+                in1=S2[j, hb][:], op0=ALU.mult, op1=ALU.add)
+            MV_USE.append(j // 2)
+            if MV_USE.count(j // 2) == 6:
+                give("mv%d" % (j // 2))
+
+        def vn(j):
+            nc.gpsimd.tensor_tensor(out=SQ[j][:], in0=MV["v", j // 2][:, :, fc(j)], in1=SQ[j][:], op=ALU.add)
+            MV_USE.append(j // 2)
+            if MV_USE.count(j // 2) == 6:
+                give("mv%d" % (j // 2))
+
+        def rs(j):
+            nc.scalar.activation(out=SQ[j][:], in_=SQ[j][:], func=ACT.Abs_reciprocal_sqrt, scale=0.6 * T / 0.16)
+
+        def mm(j):
+            rj = r_sb[:, :, 128 * j:128 * j + 128]
+            nc.vector.tensor_tensor(out=rj, in0=rj, in1=SQ[j][:], op=ALU.mult)
+            if j < NU - 1:
+                give("sq%d" % j)
+
+        def rr(j):
+            nc.vector.scalar_tensor_tensor(out=SQ[j][:], in0=w1_sb[:, :, 128 * j:128 * j + 128], scalar=0.1, in1=r_sb[:, :, 128 * j:128 * j + 128], op0=ALU.mult, op1=ALU.add)
+
+        def rn(j):
+            nc.scalar.activation(out=SQ[j][:], in_=SQ[j][:], func=ACT.Square, accum_out=stat[:, 0:1])
+
+        def wf(j):
+            WF[j] = take("small", "wf%d" % j, [P, 8, P], F32)
+            src = w1_sb[:, :, 128 * j:128 * j + 128]
+            nc.gpsimd.tensor_scalar(out=WF[j][:], in0=src, scalar1=0.2, scalar2=0.0, op0=ALU.mult, op1=ALU.add)
+
+        def nn(j):
+            if j == 0:
+                NB.append(ps.tile([P, P], F32, name="nrm", bufs=1))
+            for i in range(8):
+                rho = r_sb[:, i, 128 * j:128 * j + 128]
+                nc.tensor.matmul(out=NB[0][:], lhsT=rho, rhs=rho, start=(j == 0 and i == 0), stop=False)
+                nc.tensor.matmul(out=NB[0][:], lhsT=rho, rhs=WF[j][:, i, :], start=False, stop=(j == NU - 2 and i == 7))
+            give("wf%d" % j)
+
+        WN = {}
+
+        def wn():
+            WN["bank"] = ps.tile([P, 2, P], F32, name="tp", bufs=TB)
+            for s, units in enumerate((range(NU - 1), range(NU - 1, NU))):
+                blocks = [(i, j) for j in units for i in range(8)]
+                for n, (i, j) in enumerate(blocks):
+                    blk = w1_sb[:, i, 128 * j:128 * j + 128]
+                    nc.tensor.matmul(out=WN["bank"][:, s, :], lhsT=blk, rhs=blk, start=(n == 0), stop=(n == len(blocks) - 1))
+
+        def wt():
+            tr = keep.tile([P, 2, P], F32, name="tr")
+            for s in range(2):
+                nc.vector.tensor_tensor(out=tr[:, s, :], in0=WN["bank"][:, s, :], in1=ident[:], op=ALU.mult)
+            nc.vector.tensor_reduce(out=stat[:, 18:20], in_=tr[:], axis=AX.X, op=ALU.add)
+
+        def wt2():
+            WN["sum"] = ps.tile([P, 2], F32, name="tp", bufs=TB)
+            nc.tensor.matmul(out=WN["sum"][:], lhsT=ones[:], rhs=stat[:, 18:20], start=True, stop=True)
+
+        def wv():
+            nc.vector.tensor_reduce(out=wtot[:, 0:1], in_=WN["sum"][:], axis=AX.X, op=ALU.add)
+
+        def wr():
+            nc.scalar.activation(out=wtot[:, 1:2], in_=wtot[:, 0:1], func=ACT.Abs_reciprocal_sqrt, bias=1e-30)
+
+        def wx():
+            nc.vector.tensor_tensor(out=wtot[:, 2:3], in0=wtot[:, 0:1], in1=wtot[:, 1:2], op=ALU.mult)
+
+        def trace_rho():
+            tr = keep.tile([P, P], F32, name="tr2")
+            nc.vector.tensor_tensor(out=tr[:], in0=NB[0][:], in1=ident[:], op=ALU.mult)
+            nc.vector.tensor_reduce(out=stat[:, 1:2], in_=tr[:], axis=AX.X, op=ALU.add)
+            nc.vector.scalar_tensor_tensor(out=stat[:, 1:2], in0=stat[:, 18:19], scalar=0.01, in1=stat[:, 1:2], op0=ALU.mult, op1=ALU.add)
+
+        def tail():
+            nc.vector.tensor_tensor(out=stat[:, 17:18], in0=stat[:, 0:1], in1=stat[:, 1:2], op=ALU.add)
+            b2 = ps.tile([P, 1], F32, name="tp", bufs=TB)
+            nc.tensor.matmul(out=b2[:], lhsT=ones[:], rhs=stat[:, 17:18], start=True, stop=True)
+            nc.scalar.activation(out=wtot[:, 3:4], in_=b2[:], func=ACT.Abs_reciprocal_sqrt)
+            nc.vector.tensor_scalar(out=wtot[:, 4:5], in0=wtot[:, 3:4], scalar1=wtot[:, 2:3], scalar2=-0.5, op0=ALU.mult, op1=ALU.mult)
+            nc.vector.tensor_scalar(out=wtot[:, 5:6], in0=wtot[:, 4:5], scalar1=0.1, scalar2=1.0, op0=ALU.mult, op1=ALU.add)
+            o = out.rearrange("(i p) f -> i p f", p=P)
+            for i in range(8):
+                wa = take("big", "wa%d" % i, [P, F], F32)
+                nc.scalar.activation(out=wa[:], in_=w1_sb[:, i, :], func=ACT.Copy, scale=wtot[:, 5:6])
+                nc.vector.scalar_tensor_tensor(out=r_sb[:, i, :], in0=r_sb[:, i, :], scalar=wtot[:, 4:5], in1=wa[:], op0=ALU.mult, op1=ALU.add)
+                give("wa%d" % i)
+                nc.sync.dma_start(out=o[i], in_=r_sb[:, i, :])
+        nc.vector.memset(ones[:], 1.0)
+        nc.scalar.activation(out=wtot[:, 7:8], in_=ones[:, 0:1], func=ACT.Abs_reciprocal_sqrt)
+        make_identity(nc, ident[:])
+        nc.sync.dma_start(out=xs[:], in_=x_scale.rearrange("(g p t) o -> p g (t o)", g=NG, t=4))
+        load_x(0)
+        load_a(0, 0)
+        load_a(0, 1)
+        load_a(0, 2)
+        load_a(0, 3)
+        z(0, True, [0, 1])
+        load_raw("w2", 0)
+        xw(0, (0, 1, 2, 3), "V")
+        xi(0, 0)
+        z(1, True)
+        xi(0, 1)
+        tp("w2", 0, 0, 0)
+        tp("w2", 0, 0, 1)
+        xq(0)
+        tcopy("w2", 0, 0, 0, "V")
+        tp("w2", 0, 1, 0)
+        tcopy("w2", 0, 0, 1, "V")
+        load_raw("dy", 0)
+        z(0, True, [2, 3])
+        load_x(1)
+        tp("w2", 0, 1, 1)
+        tquant("w2", 0, 0)
+        rr_(1, True)
+        tcopy("w2", 0, 1, 0, "V")
+        tp("dy", 0, 0, 0)
+        rr_(0, True)
+        tcopy("dy", 0, 0, 0, "S")
+        tcopy("w2", 0, 1, 1, "V")
+        gl(1)
+        tp("dy", 0, 0, 1)
+        load_raw("dy", 1)
+        tp("dy", 0, 1, 0)
+        xw(1, (0, 1, 2, 3), "V")
+        load_raw("dy", 2)
+        load_x(2)
+        tcopy("dy", 0, 0, 1, "V")
+        tp("dy", 0, 1, 1)
+        tquant("dy", 0, 0)
+        tcopy("dy", 0, 1, 0, "V")
+        load_a(1)
+        tp("dy", 1, 0, 0)
+        tcopy("dy", 0, 1, 1, "V")
+        tcopy("dy", 1, 0, 0, "S")
+        tp("dy", 1, 0, 1)
+        tcopy("dy", 1, 0, 1, "S")
+        tquant("w2", 0, 1)
+        xi(1, 0)
+        tquant("dy", 0, 1)
+        tp("dy", 1, 1, 0)
+        load_raw("dy", 3)
+        gl(0)
+        tcopy("dy", 1, 1, 0, "S")
+        xw(2, (0, 1, 2, 3), "V")
+        xi(2, 0)
+        tp("dy", 1, 1, 1)
+        tp("dy", 2, 0, 0)
+        xi(2, 1)
+        ab(0)
+        tcopy("dy", 1, 1, 1, "S")
+        tcopy("dy", 2, 0, 0, "S")
+        load_x(3)
+        tquant("dy", 1, 0)
+        v1(0)
+        e(1, True)
+        tp("dy", 2, 0, 1)
+        tp("dy", 2, 1, 0)
+        tcopy("dy", 2, 0, 1, "S")
+        xi(1, 1)
+        xq(1)
+        tquant("dy", 2, 0)
+        tp("dy", 2, 1, 1)
+        tcopy("dy", 2, 1, 0, "S")
+        e(0, True)
+        tp("dy", 3, 0, 0)
+        tcopy("dy", 2, 1, 1, "S")
+        s1(0, 0)
+        ab(1)
+        tquant("dy", 1, 1)
+        tcopy("dy", 3, 0, 0, "V")
+        xq(2)
+        tp("dy", 3, 0, 1)
+        z(2, False)
+        xw(3, (0, 1, 2, 3), "V")
+        v2(0)
+        tcopy("dy", 3, 0, 1, "S")
+        v1(1)
+        s1(0, 1)
+        xi(3, 0)
+        tp("dy", 3, 1, 0)
+        tp("dy", 3, 1, 1)
+        v3(0)
+        xi(3, 1)
+        v4(0, 0)
+        load_raw("w2", 1)
+        z(3, False)
+        e(2, False)
+        xq(3)
+        tcopy("dy", 3, 1, 0, "V")
+        load_a(2)
+        tquant("dy", 2, 1)
+        e(3, False)
+        tquant("dy", 3, 0)
+        tp("w2", 1, 0, 0)
+        s1(0, 2)
+        gl(4)
+        tcopy("w2", 1, 0, 0, "V")
+        v2(1)
+        tcopy("dy", 3, 1, 1, "S")
+        v4(0, 1)
+        tp("w2", 1, 0, 1)
+        tquant("dy", 3, 1)
+        v4(0, 2)
+        tp("w2", 1, 1, 0)
+        s1(0, 3)
+        gl(5)
+        s1(1, 0)
+        gl(3)
+        tcopy("w2", 1, 0, 1, "V")
+        v3(1)
+        v4(1, 0)
+        v4(0, 3)
+        tquant("w2", 1, 0)
+        ab(5)
+        ab(4)
+        tp("w2", 1, 1, 1)
+        s1(1, 1)
+        v4(1, 1)
+        load_w1()
+        v2(2)
+        s1(1, 2)
+        gl(2)
+        q(0)
+        v2(3)
+        s1(1, 3)
+        rr_(2, False)
+        load_mv(0)
+        ab(2)
+        v4(1, 2)
+        tcopy("w2", 1, 1, 0, "V")
+        s2(0, 0)
+        s1(2, 0)
+        tcopy("w2", 1, 1, 1, "S")
+        v4(1, 3)
+        q(1)
+        v1(2)
+        sq(0, 0)
+        s2(0, 1)
+        v3(2)
+        load_a(3)
+        tquant("w2", 1, 1)
+        sq(0, 1)
+        ab(3)
+        z(4, True)
+        wn()
+        r_sb = mem.tile([P, 8, F], F32, name="r_sb", bufs=1, offset=8192 * NBIG)
+        p_(0, 0)
+        s1(2, 1)
+        s2(1, 0)
+        v4(2, 0)
+        vn(0)
+        rr_(3, False)
+        wt()
+        p_(0, 1)
+        rs(0)
+        s1(2, 2)
+        v4(2, 1)
+        v4(2, 2)
+        s1(2, 3)
+        v1(3)
+        s1(3, 0)
+        v4(2, 3)
+        s2(1, 1)
+        v3(3)
+        s1(3, 1)
+        sq(1, 0)
+        rr_(4, True)
+        s1(3, 2)
+        sq(1, 1)
+        z(5, True)
+        v4(3, 0)
+        load_mv(1)
+        rr_(5, True)
+        v4(3, 1)
+        s1(3, 3)
+        p_(1, 0)
+        q(2)
+        s1(4, 0)
+        v4(3, 2)
+        v4(3, 3)
+        p_(1, 1)
+        wf(0)
+        v1(4)
+        s2(2, 0)
+        s1(4, 1)
+        e(4, True)
+        q(3)
+        s2(2, 1)
+        mm(0)
+        sq(2, 0)
+        sq(2, 1)
+        p_(2, 0)
+        v2(4)
+        nn(0)
+        z(6, False)
+        s1(4, 2)
+        v3(4)
+        e(5, True)
+        v4(4, 0)
+        e(6, False)
+        v4(4, 1)
+        wt2()
+        v4(4, 2)
+        p_(2, 1)
+        rr_(6, False)
+        s2(3, 0)
+        v2(5)
+        sq(3, 0)
+        s2(3, 1)
+        vn(2)
+        s1(4, 3)
+        s1(5, 0)
+        v1(5)
+        p_(3, 0)
+        rs(2)
+        vn(1)
+        s1(5, 1)
+        v4(4, 3)
+        sq(3, 1)
+        s1(5, 2)
+        p_(3, 1)
+        wf(1)
+        rs(1)
+        q(4)
+        mm(2)
+        s2(4, 0)
+        load_mv(2)
+        mm(1)
+        gl(6)
+        v2(6)
+        z(7, False)
+        v3(5)
+        wf(2)
+        v4(5, 0)
+        s2(4, 1)
+        v4(5, 1)
+        sq(4, 0)
+        v4(5, 2)
+        nn(1)
+        ab(6)
+        p_(4, 0)
+        s1(5, 3)
+        vn(3)
+        s1(6, 0)
+        nn(2)
+        s1(6, 1)
+        v4(5, 3)
+        q(5)
+        gl(7)
+        e(7, False)
+        s1(6, 2)
+        sq(4, 1)
+        s2(5, 0)
+        v1(6)
+        v3(6)
+        rs(3)
+        v4(6, 0)
+        ab(7)
+        vn(4)
+        s1(6, 3)
+        v4(6, 1)
+        v4(6, 2)
+        p_(4, 1)
+        s1(7, 0)
+        wf(3)
+        s2(5, 1)
+        load_mv(3)
+        mm(3)
+        wf(4)
+        rr_(7, False)
+        rs(4)
+        nn(3)
+        sq(5, 0)
+        v4(6, 3)
+        v2(7)
+        q(6)
+        sq(5, 1)
+        v1(7)
+        p_(5, 0)
+        s1(7, 1)
+        p_(5, 1)
+        v3(7)
+        v4(7, 0)
+        s1(7, 2)
+        s2(6, 0)
+        vn(5)
+        s2(6, 1)
+        sq(6, 0)
+        sq(6, 1)
+        s1(7, 3)
+        mm(4)
+        wv()
+        v4(7, 1)
+        p_(6, 0)
+        p_(6, 1)
+        wr()
+        rs(5)
+        vn(6)
+        v4(7, 2)
+        v4(7, 3)
+        nn(4)
+        wf(6)
+        wf(5)
+        q(7)
+        s2(7, 0)
+        mm(5)
+        s2(7, 1)
+        wx()
+        sq(7, 0)
+        nn(5)
+        p_(7, 0)
+        rs(6)
+        sq(7, 1)
+        mm(6)
+        p_(7, 1)
+        vn(7)
+        rs(7)
+        mm(7)
+        nn(6)
+        rr(7)
+        rn(7)
+        trace_rho()
+        tail()

@@ -174,7 +174,7 @@ def tile_lambmlpbackwardstep_kernel(tc, x_bytes, x_scale, a, dy, w2, w1, m, v, o
         def xi(g, h):
             if h == 0:
                 XI[g] = take("big", "xi%d" % g, [P, 4096], BF16)
-            nc.vector.tensor_copy(out=XI[g][:, 2048 * h:2048 * h + 2048].rearrange("p (n t) -> p n t", t=4), in_=XW[g][:, :, 512 * h:512 * h + 512].rearrange("p t n -> p n t"))
+            nc.vector.tensor_copy(out=XI[g][:, 2048 * h:2048 * h + 2048].rearrange("p (c i t) -> p c t i", i=4, t=4), in_=XW[g][:, :, 512 * h:512 * h + 512].rearrange("p t (c i) -> p c t i", i=4))
             if h == 1:
                 give("xw%d" % g)
 
@@ -209,8 +209,8 @@ def tile_lambmlpbackwardstep_kernel(tc, x_bytes, x_scale, a, dy, w2, w1, m, v, o
             if g == 0:
                 DQ[j] = take("small", "daq%d" % j, [P, 2048], BF16)
             nc.vector.tensor_tensor(
-                out=DQ[j][:, 512 * g:512 * g + 512].rearrange("p (n t) -> p n t", t=4),
-                in0=S1[j, g][:].rearrange("p t n -> p n t"), in1=G[j][:, 4 * g:4 * g + 4, :].rearrange("p t n -> p n t"), op=ALU.mult)
+                out=DQ[j][:, 512 * g:512 * g + 512].rearrange("p (c i t) -> p c t i", i=4, t=4),
+                in0=S1[j, g][:].rearrange("p t (c i) -> p c t i", i=4), in1=G[j][:, 4 * g:4 * g + 4, :].rearrange("p t (c i) -> p c t i", i=4), op=ALU.mult)
             if g == 3:
                 give("g%d" % j)
 
@@ -248,7 +248,7 @@ def tile_lambmlpbackwardstep_kernel(tc, x_bytes, x_scale, a, dy, w2, w1, m, v, o
                 give("mv%d" % (j // 2))
 
         def vn(j):
-            nc.gpsimd.tensor_tensor(out=SQ[j][:], in0=MV["v", j // 2][:, :, fc(j)], in1=SQ[j][:], op=ALU.add)
+            nc.vector.tensor_tensor(out=SQ[j][:], in0=MV["v", j // 2][:, :, fc(j)], in1=SQ[j][:], op=ALU.add)
             MV_USE.append(j // 2)
             if MV_USE.count(j // 2) == 6:
                 give("mv%d" % (j // 2))
@@ -268,10 +268,13 @@ def tile_lambmlpbackwardstep_kernel(tc, x_bytes, x_scale, a, dy, w2, w1, m, v, o
         def rn(j):
             nc.scalar.activation(out=SQ[j][:], in_=SQ[j][:], func=ACT.Square, accum_out=stat[:, 0:1])
 
-        def wf(j):
+        def wf(j, eng):
             WF[j] = take("small", "wf%d" % j, [P, 8, P], F32)
             src = w1_sb[:, :, 128 * j:128 * j + 128]
-            nc.gpsimd.tensor_scalar(out=WF[j][:], in0=src, scalar1=0.2, scalar2=0.0, op0=ALU.mult, op1=ALU.add)
+            if eng == "S":
+                nc.scalar.activation(out=WF[j][:], in_=src, func=ACT.Copy, scale=0.2)
+            else:
+                nc.vector.tensor_scalar(out=WF[j][:], in0=src, scalar1=0.2, scalar2=None, op0=ALU.mult)
 
         def nn(j):
             if j == 0:
@@ -338,331 +341,331 @@ def tile_lambmlpbackwardstep_kernel(tc, x_bytes, x_scale, a, dy, w2, w1, m, v, o
         load_x(0)
         load_a(0, 0)
         load_a(0, 1)
+        z(0, True, [0, 1])
         load_a(0, 2)
         load_a(0, 3)
-        z(0, True, [0, 1])
-        load_raw("w2", 0)
+        z(1, True)
         xw(0, (0, 1, 2, 3), "V")
         xi(0, 0)
-        z(1, True)
         xi(0, 1)
+        z(0, True, [2, 3])
+        load_raw("w2", 0)
         tp("w2", 0, 0, 0)
-        tp("w2", 0, 0, 1)
         xq(0)
+        load_raw("dy", 0)
         tcopy("w2", 0, 0, 0, "V")
+        load_x(1)
+        rr_(1, True)
+        tp("w2", 0, 0, 1)
         tp("w2", 0, 1, 0)
         tcopy("w2", 0, 0, 1, "V")
-        load_raw("dy", 0)
-        z(0, True, [2, 3])
-        load_x(1)
+        tcopy("w2", 0, 1, 0, "V")
+        load_raw("dy", 1)
+        rr_(0, True)
         tp("w2", 0, 1, 1)
         tquant("w2", 0, 0)
-        rr_(1, True)
-        tcopy("w2", 0, 1, 0, "V")
+        tcopy("w2", 0, 1, 1, "S")
         tp("dy", 0, 0, 0)
-        rr_(0, True)
-        tcopy("dy", 0, 0, 0, "S")
-        tcopy("w2", 0, 1, 1, "V")
-        gl(1)
-        tp("dy", 0, 0, 1)
-        load_raw("dy", 1)
-        tp("dy", 0, 1, 0)
         xw(1, (0, 1, 2, 3), "V")
-        load_raw("dy", 2)
-        load_x(2)
-        tcopy("dy", 0, 0, 1, "V")
-        tp("dy", 0, 1, 1)
-        tquant("dy", 0, 0)
-        tcopy("dy", 0, 1, 0, "V")
-        load_a(1)
-        tp("dy", 1, 0, 0)
-        tcopy("dy", 0, 1, 1, "V")
-        tcopy("dy", 1, 0, 0, "S")
-        tp("dy", 1, 0, 1)
-        tcopy("dy", 1, 0, 1, "S")
-        tquant("w2", 0, 1)
-        xi(1, 0)
-        tquant("dy", 0, 1)
-        tp("dy", 1, 1, 0)
-        load_raw("dy", 3)
         gl(0)
-        tcopy("dy", 1, 1, 0, "S")
+        load_raw("dy", 2)
+        tp("dy", 0, 0, 1)
+        tcopy("dy", 0, 0, 0, "V")
+        xi(1, 0)
+        tcopy("dy", 0, 0, 1, "S")
+        tquant("w2", 0, 1)
+        tp("dy", 0, 1, 0)
+        tp("dy", 0, 1, 1)
+        tcopy("dy", 0, 1, 0, "S")
+        xi(1, 1)
+        load_x(2)
+        tp("dy", 1, 0, 0)
         xw(2, (0, 1, 2, 3), "V")
-        xi(2, 0)
-        tp("dy", 1, 1, 1)
-        tp("dy", 2, 0, 0)
-        xi(2, 1)
+        tcopy("dy", 0, 1, 1, "V")
+        xq(1)
+        tp("dy", 1, 0, 1)
         ab(0)
+        tcopy("dy", 1, 0, 0, "S")
+        load_a(1)
+        tp("dy", 1, 1, 0)
+        tquant("dy", 0, 0)
+        xi(2, 0)
+        v1(0)
+        gl(1)
+        load_raw("dy", 3)
+        gl(3)
+        tcopy("dy", 1, 0, 1, "V")
+        tcopy("dy", 1, 1, 0, "S")
+        tp("dy", 1, 1, 1)
+        gl(2)
+        xi(2, 1)
+        tquant("dy", 0, 1)
+        load_x(3)
+        tp("dy", 2, 0, 0)
         tcopy("dy", 1, 1, 1, "S")
         tcopy("dy", 2, 0, 0, "S")
-        load_x(3)
+        load_raw("w2", 1)
+        xw(3, (0, 1, 2, 3), "V")
+        z(3, False)
         tquant("dy", 1, 0)
-        v1(0)
-        e(1, True)
+        xi(3, 0)
+        tquant("dy", 1, 1)
         tp("dy", 2, 0, 1)
         tp("dy", 2, 1, 0)
         tcopy("dy", 2, 0, 1, "S")
-        xi(1, 1)
-        xq(1)
-        tquant("dy", 2, 0)
-        tp("dy", 2, 1, 1)
         tcopy("dy", 2, 1, 0, "S")
-        e(0, True)
+        tp("dy", 2, 1, 1)
+        tcopy("dy", 2, 1, 1, "V")
         tp("dy", 3, 0, 0)
-        tcopy("dy", 2, 1, 1, "S")
-        s1(0, 0)
-        ab(1)
-        tquant("dy", 1, 1)
-        tcopy("dy", 3, 0, 0, "V")
-        xq(2)
+        e(0, True)
         tp("dy", 3, 0, 1)
-        z(2, False)
-        xw(3, (0, 1, 2, 3), "V")
-        v2(0)
-        tcopy("dy", 3, 0, 1, "S")
-        v1(1)
-        s1(0, 1)
-        xi(3, 0)
-        tp("dy", 3, 1, 0)
-        tp("dy", 3, 1, 1)
-        v3(0)
+        s1(0, 0)
+        tcopy("dy", 3, 0, 0, "S")
         xi(3, 1)
-        v4(0, 0)
-        load_raw("w2", 1)
-        z(3, False)
-        e(2, False)
-        xq(3)
-        tcopy("dy", 3, 1, 0, "V")
-        load_a(2)
-        tquant("dy", 2, 1)
         e(3, False)
-        tquant("dy", 3, 0)
+        xq(2)
+        tquant("dy", 2, 0)
+        load_a(2)
+        xq(3)
+        tp("dy", 3, 1, 0)
+        tcopy("dy", 3, 0, 1, "V")
+        tcopy("dy", 3, 1, 0, "S")
+        e(1, True)
+        tp("dy", 3, 1, 1)
+        tcopy("dy", 3, 1, 1, "S")
+        v2(0)
+        s1(0, 1)
+        tquant("dy", 2, 1)
+        ab(1)
         tp("w2", 1, 0, 0)
         s1(0, 2)
-        gl(4)
-        tcopy("w2", 1, 0, 0, "V")
-        v2(1)
-        tcopy("dy", 3, 1, 1, "S")
-        v4(0, 1)
-        tp("w2", 1, 0, 1)
-        tquant("dy", 3, 1)
-        v4(0, 2)
-        tp("w2", 1, 1, 0)
-        s1(0, 3)
-        gl(5)
-        s1(1, 0)
-        gl(3)
-        tcopy("w2", 1, 0, 1, "V")
-        v3(1)
-        v4(1, 0)
-        v4(0, 3)
-        tquant("w2", 1, 0)
-        ab(5)
-        ab(4)
-        tp("w2", 1, 1, 1)
-        s1(1, 1)
-        v4(1, 1)
+        tcopy("w2", 1, 0, 0, "S")
+        v3(0)
         load_w1()
-        v2(2)
-        s1(1, 2)
-        gl(2)
-        q(0)
+        tquant("dy", 3, 0)
+        v4(0, 0)
+        z(2, False)
+        tquant("dy", 3, 1)
+        s1(0, 3)
+        tp("w2", 1, 0, 1)
+        v4(0, 1)
+        tcopy("w2", 1, 0, 1, "S")
+        v1(1)
+        v2(1)
+        s1(1, 0)
+        tp("w2", 1, 1, 0)
+        tp("w2", 1, 1, 1)
+        e(2, False)
+        tcopy("w2", 1, 1, 0, "S")
         v2(3)
-        s1(1, 3)
-        rr_(2, False)
+        v4(0, 2)
+        v3(1)
         load_mv(0)
+        v4(0, 3)
         ab(2)
-        v4(1, 2)
-        tcopy("w2", 1, 1, 0, "V")
+        s1(1, 1)
+        v4(1, 0)
+        q(0)
+        v4(1, 1)
+        rr_(2, False)
+        ab(3)
+        s1(1, 2)
+        s1(1, 3)
         s2(0, 0)
-        s1(2, 0)
+        load_a(3)
+        tquant("w2", 1, 0)
         tcopy("w2", 1, 1, 1, "S")
-        v4(1, 3)
-        q(1)
-        v1(2)
+        rr_(3, False)
+        v4(1, 2)
         sq(0, 0)
         s2(0, 1)
-        v3(2)
-        load_a(3)
-        tquant("w2", 1, 1)
-        sq(0, 1)
-        ab(3)
+        v1(2)
+        v2(2)
         z(4, True)
         wn()
+        v4(1, 3)
+        tquant("w2", 1, 1)
+        v3(2)
         r_sb = mem.tile([P, 8, F], F32, name="r_sb", bufs=1, offset=8192 * NBIG)
         p_(0, 0)
+        s1(2, 0)
         s1(2, 1)
-        s2(1, 0)
-        v4(2, 0)
-        vn(0)
-        rr_(3, False)
-        wt()
-        p_(0, 1)
-        rs(0)
+        sq(0, 1)
+        q(1)
         s1(2, 2)
-        v4(2, 1)
-        v4(2, 2)
+        v4(2, 0)
         s1(2, 3)
-        v1(3)
-        s1(3, 0)
-        v4(2, 3)
-        s2(1, 1)
-        v3(3)
-        s1(3, 1)
-        sq(1, 0)
+        vn(0)
         rr_(4, True)
-        s1(3, 2)
-        sq(1, 1)
+        v1(3)
+        v4(2, 1)
+        v3(3)
+        v4(2, 2)
+        wt()
         z(5, True)
-        v4(3, 0)
+        s2(1, 0)
+        p_(0, 1)
+        s1(3, 0)
         load_mv(1)
-        rr_(5, True)
+        e(4, True)
+        v4(3, 0)
+        v4(2, 3)
+        wf(0, "V")
+        s2(1, 1)
+        sq(1, 0)
+        s1(3, 1)
+        gl(4)
+        s1(3, 2)
+        gl(5)
+        sq(1, 1)
+        p_(1, 0)
         v4(3, 1)
         s1(3, 3)
-        p_(1, 0)
-        q(2)
-        s1(4, 0)
-        v4(3, 2)
-        v4(3, 3)
         p_(1, 1)
-        wf(0)
-        v1(4)
-        s2(2, 0)
+        v4(3, 2)
+        q(2)
+        ab(4)
+        s1(4, 0)
         s1(4, 1)
-        e(4, True)
+        v4(3, 3)
+        gl(6)
+        v2(4)
+        s2(2, 0)
+        sq(2, 0)
+        v1(4)
+        rs(0)
+        wt2()
         q(3)
         s2(2, 1)
-        mm(0)
-        sq(2, 0)
-        sq(2, 1)
-        p_(2, 0)
-        v2(4)
-        nn(0)
-        z(6, False)
-        s1(4, 2)
-        v3(4)
-        e(5, True)
-        v4(4, 0)
-        e(6, False)
-        v4(4, 1)
-        wt2()
-        v4(4, 2)
-        p_(2, 1)
-        rr_(6, False)
-        s2(3, 0)
-        v2(5)
-        sq(3, 0)
-        s2(3, 1)
-        vn(2)
-        s1(4, 3)
-        s1(5, 0)
-        v1(5)
-        p_(3, 0)
-        rs(2)
         vn(1)
+        sq(2, 1)
+        s1(4, 2)
+        p_(2, 0)
+        rr_(5, True)
+        mm(0)
+        v3(4)
+        vn(2)
+        v4(4, 0)
+        rs(1)
+        s2(3, 0)
+        e(5, True)
+        p_(2, 1)
+        ab(5)
+        mm(1)
+        nn(0)
+        wf(1, "V")
+        s1(4, 3)
+        z(7, False)
+        v4(4, 1)
+        s2(3, 1)
+        v1(5)
+        v4(4, 2)
+        sq(3, 0)
+        p_(3, 0)
+        v2(5)
+        wv()
+        v3(5)
+        s1(5, 0)
+        nn(1)
+        z(6, False)
+        sq(3, 1)
         s1(5, 1)
         v4(4, 3)
-        sq(3, 1)
-        s1(5, 2)
-        p_(3, 1)
-        wf(1)
-        rs(1)
-        q(4)
-        mm(2)
-        s2(4, 0)
-        load_mv(2)
-        mm(1)
-        gl(6)
-        v2(6)
-        z(7, False)
-        v3(5)
-        wf(2)
-        v4(5, 0)
-        s2(4, 1)
-        v4(5, 1)
-        sq(4, 0)
-        v4(5, 2)
-        nn(1)
+        e(6, False)
         ab(6)
-        p_(4, 0)
-        s1(5, 3)
-        vn(3)
-        s1(6, 0)
-        nn(2)
-        s1(6, 1)
-        v4(5, 3)
-        q(5)
-        gl(7)
+        load_mv(2)
+        v4(5, 0)
+        q(4)
+        s2(4, 0)
         e(7, False)
-        s1(6, 2)
-        sq(4, 1)
-        s2(5, 0)
+        p_(3, 1)
+        rr_(6, False)
+        v4(5, 1)
+        wr()
+        rs(2)
+        v2(6)
+        s1(5, 2)
+        v4(5, 2)
+        s1(5, 3)
+        s1(6, 0)
+        vn(3)
+        wf(2, "S")
+        sq(4, 0)
+        v4(5, 3)
         v1(6)
-        v3(6)
-        rs(3)
-        v4(6, 0)
-        ab(7)
-        vn(4)
-        s1(6, 3)
-        v4(6, 1)
-        v4(6, 2)
-        p_(4, 1)
-        s1(7, 0)
-        wf(3)
-        s2(5, 1)
-        load_mv(3)
-        mm(3)
-        wf(4)
         rr_(7, False)
-        rs(4)
-        nn(3)
-        sq(5, 0)
+        s1(6, 1)
+        s2(4, 1)
+        mm(2)
+        v3(6)
+        q(5)
+        sq(4, 1)
+        v4(6, 0)
+        vn(4)
+        s1(6, 2)
+        nn(2)
+        v4(6, 1)
+        rs(3)
+        wf(3, "S")
+        s1(6, 3)
+        p_(4, 0)
+        mm(3)
+        gl(7)
+        v4(6, 2)
+        s1(7, 0)
+        p_(4, 1)
+        s2(5, 0)
+        load_mv(3)
         v4(6, 3)
         v2(7)
+        sq(5, 0)
+        s1(7, 1)
+        s2(5, 1)
+        ab(7)
+        p_(5, 0)
+        s1(7, 2)
+        nn(3)
         q(6)
         sq(5, 1)
+        rs(4)
         v1(7)
-        p_(5, 0)
-        s1(7, 1)
         p_(5, 1)
-        v3(7)
-        v4(7, 0)
-        s1(7, 2)
         s2(6, 0)
-        vn(5)
-        s2(6, 1)
         sq(6, 0)
+        wf(4, "S")
+        s2(6, 1)
+        v3(7)
+        wx()
         sq(6, 1)
-        s1(7, 3)
+        v4(7, 0)
         mm(4)
-        wv()
-        v4(7, 1)
         p_(6, 0)
-        p_(6, 1)
-        wr()
-        rs(5)
-        vn(6)
+        s1(7, 3)
+        v4(7, 1)
+        vn(5)
         v4(7, 2)
+        rs(5)
+        wf(5, "S")
         v4(7, 3)
         nn(4)
-        wf(6)
-        wf(5)
         q(7)
-        s2(7, 0)
         mm(5)
-        s2(7, 1)
-        wx()
+        p_(6, 1)
+        s2(7, 0)
         sq(7, 0)
+        s2(7, 1)
+        vn(6)
         nn(5)
-        p_(7, 0)
-        rs(6)
         sq(7, 1)
-        mm(6)
+        p_(7, 0)
+        wf(6, "V")
         p_(7, 1)
         vn(7)
+        rs(6)
+        mm(6)
+        nn(6)
         rs(7)
         mm(7)
-        nn(6)
         rr(7)
         rn(7)
         trace_rho()

@@ -1,672 +1,582 @@
-from contextlib import ExitStack
 import math
+from contextlib import ExitStack
+
 import concourse.mybir as mybir
 from concourse.masks import make_identity
 
-T, D, F = 2048, 1024, 1024
+TOKENS, WIDTH, HIDDEN = 2048, 1024, 1024
+
 F32 = mybir.dt.float32
 BF16 = mybir.dt.bfloat16
 U32 = mybir.dt.uint32
 U8 = mybir.dt.uint8
 FP8 = mybir.dt.float8_e4m3fn
-X4 = mybir.dt.float8_e4m3fn_x4
+FP8X4 = mybir.dt.float8_e4m3fn_x4
 ACT = mybir.ActivationFunctionType
 ALU = mybir.AluOpType
-AX = mybir.AxisListType
+AXIS = mybir.AxisListType
+
 P = 128
-NG = 4
-NU = 8
-FLOPS = 2 * 2 * T * D * F + 40 * T * F
-DELTA = 2.0 ** -60
+PACK = 4
+PASS = P * PACK
+TOKEN_PASSES = TOKENS // PASS
+WIDTH_PASSES = WIDTH // PASS
+ROW_TILES = WIDTH // P
+UNITS = HIDDEN // P
+LAST = UNITS - 1
+
+DELTA = 2.0**-60
 INV_SQRT_2PI = 1.0 / math.sqrt(2.0 * math.pi)
+
+FLOPS = 2 * 2 * TOKENS * WIDTH * HIDDEN
+
+BIG, RAW, SMALL = 14, 4, 5
+BIG_BYTES, SMALL_BYTES = 8192, 4096
+
+TURN_BANKS, DH_BANKS, G_BANKS = 2, 3, 2
+
+ORDER = """
+x.0.0 a.0.0 xw.0.0 x.0.1 a.0.1 a.0.2 a.0.3 w2.0 xw.0.1 xi.0.0 xi.0.1 xq.0 z.0.0 dy.0 z.0.1
+x.1 z.1 dy.1 cv.4.0.0 cv.4.0.1 tq.4.0 cv.4.1.0 r.0 xw.1 cv.0.0.0 xi.1.0 r.1 cs.4.1.1 dy.2 cv.0.0.1
+xi.1.1 cv.0.1.0 x.2 tq.4.1 ge.1 ge.0 cs.1.0.0 cv.0.1.1 ab.0 xw.2 cs.1.0.1 cv.1.1.0 tq.0.0 cdf.0 xq.1
+ab.1 cs.1.1.1 tq.1.0 a.1 cs.2.0.0 ge.2 tq.0.1 cv.2.0.1 e.0 dy.3 xi.2.0 x.3 cv.2.1.0 xw.3 z.2
+tq.2.0 cs.3.0.0 xi.3.0 ab.2 cv.2.1.1 tq.1.1 z.3 ph.0 xi.2.1 cs.3.0.1 e.1 xi.3.1 cv.3.1.0 gp.0 w2.1
+cs.3.1.1 tq.3.0 e.3 a.2 da.0.0 tq.2.1 tq.3.1 cv.5.0.0 da.0.1 e.2 xq.2 cdf.1 ph.1 r.3 da.0.2
+cv.5.0.1 r.2 z.5 ph.2 gp.1 cs.5.1.0 da.0.3 r.5 z.4 tq.5.0 xq.3 da.1.0 e.4 cdf.2 e.5
+ge.3 da.1.1 gp.2 da.1.2 w1 qd.0 cv.5.1.1 da.2.0 da.1.3 mv.0 da.2.1 sq.0.0 ph.3 ge.5 qd.1
+tq.5.1 wm sq.0.1 da.2.2 ph.4 m2.0 ab.3 m1.0.0 da.2.3 m1.0.1 ph.5 ge.4 a.3 cdf.3 rs.0
+mv.1 sq.1.0 rho.0 wf.0 nm.0 gp.3 sq.1.1 m1.1.0 m2.1 da.3.0 r.4 qd.2 da.3.1 m1.1.1 ab.4
+da.3.2 ab.5 cdf.4 rs.1 sq.2.0 wf.1 da.3.3 rho.1 z.6 m1.2.0 nm.1 sq.2.1 gp.4 mv.2 r.6
+m2.2 da.4.0 qd.3 wf.2 rs.2 e.6 da.4.1 sq.3.0 m1.2.1 cdf.5 da.4.2 rho.2 ge.6 gp.5 mv.3
+nm.2 ph.6 da.4.3 da.5.0 sq.3.1 m2.3 m1.3.0 qd.4 ge.7 rs.3 da.5.1 sq.4.0 ab.6 m1.3.1 da.5.2
+wd sq.4.1 wt da.5.3 rho.3 wf.3 m1.4.0 qd.5 z.7 sq.5.0 cdf.6 m2.4 r.7 rs.4 nm.3
+gp.6 m1.5.0 da.6.0 ab.7 wf.4 m1.4.1 da.6.1 rho.4 da.6.2 sq.5.1 nm.4 cdf.7 e.7 da.6.3 wf.6
+m1.5.1 wf.5 qd.6 m2.5 rs.5 ph.7 sq.6.0 gp.7 sq.6.1 ws da.7.0 rho.5 nm.5 m2.6.1 m2.6.0
+rs.6.1 m1.6.0 da.7.1 rs.6.0 da.7.2 m1.6.1 da.7.3 qd.7 wr sq.7.0 rho.6.0 rho.6.1 m2.7.0 m1.7.0 sq.7.1
+rs.7.0 m2.7.1 wn rs.7.1 rho.7.0 nm.6.0 m1.7.1 rho.7.1 nm.6.1 lr.0 lr.1 rd lq.1 lq.0
+""".split()
 
 
 def tile_lambmlpbackwardstep_kernel(tc, x_bytes, x_scale, a, dy, w2, w1, m, v, out):
     nc = tc.nc
     with ExitStack() as ctx:
-        TB, DB = 2, 3
-        NBIG, NSMALL = 13, 5
-        SLOTS = {
-            "big": [8192 * s for s in range(NBIG)],
-            "turn": [8192 * (NBIG + s) for s in range(4)],
-            "small": [8192 * (NBIG + 4) + 4096 * s for s in range(NSMALL)],
-        }
-        OFF = {}
-        WF, NB, A_USE, MV_USE = {}, [], [], []
         keep = ctx.enter_context(tc.tile_pool(name="keep", bufs=1))
         mem = ctx.enter_context(tc.tile_pool(name="mem", bufs=1))
-        ps = ctx.enter_context(tc.psum_pool(name="ps", bufs=2))
+        psum = ctx.enter_context(tc.psum_pool(name="psum", bufs=2))
         ctx.enter_context(tc.manual_schedule())
 
-        ident = keep.tile([P, P], F32, name="ident")
+        identity = keep.tile([P, P], F32, name="identity")
         ones = keep.tile([P, P], F32, name="ones")
-        xs = keep.tile([P, NG, 4], F32, name="xs")
-        x_codes = keep.tile([P, NG, D], U32, name="x_codes", align_bytes=64)
-        x_planes = keep.tile([P, NG, D], U8, name="x_planes", align_bytes=64)
-        dy_codes = keep.tile([P, 2, T], U32, name="dy_codes", align_bytes=64)
-        dy_planes = keep.tile([P, 2, T], U8, name="dy_planes", align_bytes=64)
-        w2_codes = keep.tile([P, 2, F], U32, name="w2_codes", align_bytes=64)
-        w2_planes = keep.tile([P, 2, F], U8, name="w2_planes", align_bytes=64)
-        w1_sb = keep.tile([P, 8, F], BF16, name="w1_sb")
-        stat = keep.tile([P, 32], F32, name="stat")
-        wtot = keep.tile([P, 8], F32, name="wtot")
+        x_scales = keep.tile([P, TOKEN_PASSES, PACK], F32, name="x_scales")
+        x_codes = keep.tile([P, TOKEN_PASSES, WIDTH], U32, name="x_codes", align_bytes=64)
+        x_mx_scales = keep.tile([P, TOKEN_PASSES, WIDTH], U8, name="x_mx_scales", align_bytes=64)
+        dy_codes = keep.tile([P, WIDTH_PASSES, TOKENS], U32, name="dy_codes", align_bytes=64)
+        dy_mx_scales = keep.tile([P, WIDTH_PASSES, TOKENS], U8, name="dy_mx_scales", align_bytes=64)
+        w2_codes = keep.tile([P, WIDTH_PASSES, HIDDEN], U32, name="w2_codes", align_bytes=64)
+        w2_mx_scales = keep.tile([P, WIDTH_PASSES, HIDDEN], U8, name="w2_mx_scales", align_bytes=64)
+        w1_tile = keep.tile([P, ROW_TILES, HIDDEN], BF16, name="w1_tile")
+        diagonal = keep.tile([P, 2, P], F32, name="diagonal")
+        sums = keep.tile([P, 8], F32, name="sums")
+        w1_norm = keep.tile([P, 8], F32, name="w1_norm")
+        trust = keep.tile([P, 8], F32, name="trust")
 
-        A, XB, RAW, MV = {}, {}, {}, {}
-        R, E, G, GRP, XW, XI, DQ, DC, DPL, S2, SQ, S1 = ({} for n in range(12))
+        free = {
+            "big": [BIG_BYTES * s for s in range(BIG)],
+            "raw": [BIG_BYTES * (BIG + s) for s in range(RAW)],
+            "small": [BIG_BYTES * (BIG + RAW) + SMALL_BYTES * s for s in range(SMALL)],
+        }
+        owner = {}
 
         def take(kind, name, shape, dtype):
-            OFF[name] = (kind, SLOTS[kind].pop(0))
-            return mem.tile(shape, dtype, name=name, bufs=1, offset=OFF[name][1], align_bytes=64)
+            owner[name] = (kind, free[kind].pop(0))
+            return mem.tile(shape, dtype, name=name, bufs=1, offset=owner[name][1], align_bytes=64)
 
         def give(name):
-            kind, off = OFF.pop(name)
-            SLOTS[kind].append(off)
+            kind, offset = owner.pop(name)
+            free[kind].append(offset)
 
-        def load_a(i, g=None):
-            if i not in A:
-                A[i] = take("big", "a%d" % i, [P, 16, 256], BF16)
-            src = a.rearrange("(g p t) f -> p g t f", g=NG, t=4)
-            gs = range(NG) if g is None else [g]
-            for q in gs:
-                nc.sync.dma_start(out=A[i][:, 4 * q:4 * q + 4, :], in_=src[:, q, :, 256 * i:256 * (i + 1)])
+        done = set()
+        tiles = {}
 
-        def load_x(g):
-            XB[g] = take("small", "xb%d" % g, [P, 4, D], U8)
-            nc.sync.dma_start(out=XB[g][:], in_=x_bytes.rearrange("(g p t) d -> g p t d", g=NG, t=4)[g])
 
-        def load_raw(kind, q):
-            t = take("turn", "raw%s%d" % (kind, q), [P, 4, D], BF16)
-            RAW[kind, q] = t
-            if kind == "dy":
-                src = dy.rearrange("(g p t) k -> g p t k", g=NG, t=4)[q]
-            else:
-                src = w2.rearrange("(h b p) k -> h p b k", h=2, b=4)[q]
-            nc.sync.dma_start(out=t[:], in_=src)
+        def load_a(pair, g=None):
+            if ("a", pair) not in tiles:
+                tiles["a", pair] = take("big", "a%d" % pair, [P, TOKEN_PASSES * PACK, 2 * P], BF16)
+            source = a.rearrange("(g p t) f -> p g t f", g=TOKEN_PASSES, t=PACK)
+            for q in range(TOKEN_PASSES) if g is None else (g,):
+                nc.sync.dma_start(
+                    out=tiles["a", pair][:, PACK * q : PACK * q + PACK, :],
+                    in_=source[:, q, :, 2 * P * pair : 2 * P * (pair + 1)],
+                )
 
-        def load_mv(i):
-            t = take("big", "mv%d" % i, [P, 16, 256], BF16)
-            for n, (k, src) in enumerate((("m", m), ("v", v))):
-                MV[k, i] = t[:, 8 * n:8 * n + 8, :]
-                nc.sync.dma_start(out=MV[k, i], in_=src.rearrange("(i p) f -> p i f", p=P)[:, :, 256 * i:256 * (i + 1)])
+        def load_x(g, half=None):
+            if ("x", g) not in tiles:
+                tiles["x", g] = take("small", "x_raw%d" % g, [P, PACK, WIDTH], U8)
+            ts = slice(0, PACK) if half is None else slice(2 * half, 2 * half + 2)
+            source = x_bytes.rearrange("(g p t) d -> g p t d", g=TOKEN_PASSES, t=PACK)
+            nc.sync.dma_start(out=tiles["x", g][:, ts, :], in_=source[g][:, ts, :])
+
+        def load_dy(g):
+            tiles["rows", g] = take("raw", "dy_rows%d" % g, [P, PACK, WIDTH], BF16)
+            source = dy.rearrange("(g p t) k -> g p t k", g=TOKEN_PASSES, t=PACK)
+            nc.sync.dma_start(out=tiles["rows", g][:], in_=source[g])
+
+        def load_w2(half):
+            index = TOKEN_PASSES + half
+            tiles["rows", index] = take("raw", "w2_rows%d" % half, [P, 4, WIDTH], BF16)
+            source = w2.rearrange("(h b p) k -> h p b k", h=2, b=4)
+            nc.sync.dma_start(out=tiles["rows", index][:], in_=source[half])
+
+        def load_moments(pair):
+            both = take("big", "moments%d" % pair, [P, 2 * ROW_TILES, 2 * P], BF16)
+            for n, source in enumerate((m, v)):
+                tiles["mv"[n], pair] = both[:, ROW_TILES * n : ROW_TILES * (n + 1), :]
+                nc.sync.dma_start(
+                    out=tiles["mv"[n], pair],
+                    in_=source.rearrange("(i p) f -> p i f", p=P)[:, :, 2 * P * pair : 2 * P * (pair + 1)],
+                )
 
         def load_w1():
-            nc.sync.dma_start(out=w1_sb[:], in_=w1.rearrange("(i p) f -> p i f", p=P))
+            nc.sync.dma_start(out=w1_tile[:], in_=w1.rearrange("(i p) f -> p i f", p=P))
 
-        def done_a(j):
-            A_USE.append(j // 2)
-            if A_USE.count(j // 2) == 4:
-                give("a%d" % (j // 2))
+
+        def widen_x(g, half=None):
+            if half in (None, 0):
+                tiles["pairs", g] = take("big", "x_pairs%d" % g, [P, 2, WIDTH, 2], BF16)
+            for t in range(PACK) if half is None else (2 * half, 2 * half + 1):
+                nc.vector.tensor_scalar(
+                    out=tiles["pairs", g][:, t // 2, :, t % 2],
+                    in0=tiles["x", g][:, t, :].bitcast(FP8),
+                    scalar1=x_scales[:, g, t : t + 1],
+                    scalar2=None,
+                    op0=ALU.mult,
+                )
+            if half in (None, 1):
+                give("x_raw%d" % g)
+
+        def interleave_x(g, half):
+            if half == 0:
+                tiles["x_bf16", g] = take("big", "x_bf16%d" % g, [P, PACK * WIDTH], BF16)
+            n = WIDTH // 2
+            words = tiles["pairs", g][:].rearrange("p u n e -> p (u n e)").bitcast(F32)
+            nc.vector.tensor_copy(
+                out=tiles["x_bf16", g][:, PACK * n * half : PACK * n * (half + 1)]
+                .bitcast(F32)
+                .rearrange("p (n u) -> p n u", u=2),
+                in_=words.rearrange("p (u n) -> p n u", u=2)[:, n * half : n * (half + 1), :],
+            )
+            if half == 1:
+                give("x_pairs%d" % g)
+
+        def quantise_x(g):
+            nc.vector.quantize_mx(
+                out=x_codes[:, g, :].bitcast(FP8X4), scales=x_mx_scales[:, g, :], in_=tiles["x_bf16", g][:]
+            )
+            give("x_bf16%d" % g)
+
+
+        def turn(index, c, b):
+            bank = psum.tile([P, 2, 2, P], F32, name="turned", bufs=TURN_BANKS)
+            tiles["turned", index, c, b] = bank
+            for k in range(2):
+                words = tiles["rows", index][:, 2 * b + k, :].bitcast(F32)
+                for u in range(2):
+                    nc.tensor.transpose(
+                        out=bank[:, k, u, :],
+                        in_=words[:, PASS // 2 * c + u : PASS // 2 * (c + 1) : 2],
+                        identity=identity[:],
+                    )
+
+        def copy_turned(index, c, b, on_scalar):
+            name = "turned%d%d" % (index, c)
+            if b == 0:
+                tiles["grouped", index, c] = take("small", name, [P, PACK * PASS], BF16)
+            out_words = tiles["grouped", index, c][:].bitcast(F32)[:, PASS * b : PASS * (b + 1)]
+            out_words = out_words.rearrange("p (k r u) -> p k r u", k=2, u=2)
+            in_words = tiles["turned", index, c, b][:].rearrange("p k u r -> p k r u")
+            if on_scalar:
+                nc.scalar.copy(out=out_words, in_=in_words)
+            else:
+                nc.vector.tensor_copy(out=out_words, in_=in_words)
+            done.add("copied.%d.%d.%d" % (index, c, b))
+
+        def copy_on_scalar(index, c, b):
+            copy_turned(index, c, b, True)
+
+        def copy_on_vector(index, c, b):
+            copy_turned(index, c, b, False)
+
+        def quantise_turned(index, c):
+            if index < TOKEN_PASSES:
+                codes, scales, first = dy_codes, dy_mx_scales, PASS * index
+            else:
+                codes, scales, first = w2_codes, w2_mx_scales, PASS * (index - TOKEN_PASSES)
+            columns = slice(first, first + PASS)
+            nc.vector.quantize_mx(
+                out=codes[:, c, columns].bitcast(FP8X4),
+                scales=scales[:, c, columns],
+                in_=tiles["grouped", index, c][:],
+            )
+            give("turned%d%d" % (index, c))
+            if c == WIDTH_PASSES - 1:
+                give(("dy_rows%d" % index) if index < TOKEN_PASSES else ("w2_rows%d" % (index - TOKEN_PASSES)))
+
+
+        uses_of_a = []
 
         def a_unit(j):
-            return A[j // 2][:, :, 128 * (j % 2):128 * (j % 2) + 128]
+            return tiles["a", j // 2][:, :, P * (j % 2) : P * (j % 2) + P]
 
-        def z(j, first, gs=None):
-            d = E if first else R
-            if j not in d:
-                d[j] = take("big", ("e%d" if first else "r%d") % j, [P, 16, P], F32)
-            sl = slice(0, 16) if gs is None else slice(4 * gs[0], 4 * gs[-1] + 4)
-            nc.scalar.activation(out=d[j][:, sl, :], in_=a_unit(j)[:, sl, :], func=ACT.Square)
+        def used_a(j):
+            uses_of_a.append(j // 2)
+            if uses_of_a.count(j // 2) == 4:
+                give("a%d" % (j // 2))
 
-        def rr_(j, first):
-            if first:
-                R[j] = take("big", "r%d" % j, [P, 16, P], F32)
-                src = E[j]
-            else:
-                src = R[j]
-            nc.scalar.activation(out=R[j][:], in_=src[:], func=ACT.Abs_reciprocal_sqrt, bias=DELTA * DELTA)
+        def unit_tile(what, j):
+            tiles[what, j] = take("big", "%s%d" % (what, j), [P, TOKEN_PASSES * PACK, P], F32)
+            return tiles[what, j]
 
-        def e(j, first):
-            if first:
-                src = E[j]
-            else:
-                E[j] = take("big", "e%d" % j, [P, 16, P], F32)
-                src = R[j]
-            nc.scalar.activation(out=E[j][:], in_=src[:], func=ACT.Exp, scale=-0.5)
+        def square_a(j, half=None):
+            z = unit_tile("z", j) if half in (None, 0) else tiles["z", j]
+            part = slice(0, 16) if half is None else slice(8 * half, 8 * half + 8)
+            nc.scalar.activation(out=z[:, part, :], in_=a_unit(j)[:, part, :], func=ACT.Square)
 
-        def gl(j):
-            G[j] = take("big", "g%d" % j, [P, 16, P], F32)
-            nc.scalar.activation(out=G[j][:], in_=a_unit(j), func=ACT.Gelu, bias=DELTA)
-            done_a(j)
+        def rsqrt_z(j):
+            z = tiles["z", j]
+            tiles["root", j] = z if ("gauss", j) in tiles else unit_tile("root", j)
+            nc.scalar.activation(
+                out=tiles["root", j][:], in_=z[:], func=ACT.Abs_reciprocal_sqrt, bias=DELTA * DELTA
+            )
 
-        def ab(j):
-            nc.scalar.activation(out=G[j][:], in_=G[j][:], func=ACT.Abs)
+        def exp_z(j):
+            z = tiles["z", j]
+            tiles["gauss", j] = z if ("root", j) in tiles else unit_tile("gauss", j)
+            nc.scalar.activation(out=tiles["gauss", j][:], in_=z[:], func=ACT.Exp, scale=-0.5)
 
-        BK = {}
+        def give_unit(what, j):
+            give("%s%d" % ("z" if tiles[what, j] is tiles["z", j] else what, j))
 
-        def tp(kind, q, c, b):
-            bank = ps.tile([P, 2, 2, P], F32, name="tp", bufs=TB)
-            BK[kind, q, c, b] = bank
-            for k in range(2):
-                w = RAW[kind, q][:, 2 * b + k, :].bitcast(F32)
-                for u in range(2):
-                    nc.tensor.transpose(out=bank[:, k, u, :], in_=w[:, 256 * c + u:256 * (c + 1):2], identity=ident[:])
+        def gelu_a(j):
+            nc.scalar.activation(out=unit_tile("gelu", j)[:], in_=a_unit(j), func=ACT.Gelu, bias=DELTA)
+            used_a(j)
 
-        def tcopy(kind, q, c, b, eng):
-            if b == 0:
-                GRP[kind, q, c] = take("small", "grp%s%d%d" % (kind, q, c), [P, 2048], BF16)
-            dst = GRP[kind, q, c][:].bitcast(F32)[:, 512 * b:512 * b + 512].rearrange("p (j r u) -> p j r u", j=2, u=2)
-            src = BK[kind, q, c, b][:].rearrange("p j u r -> p j r u")
-            if eng == "S":
-                nc.scalar.copy(out=dst, in_=src)
-            else:
-                nc.vector.tensor_copy(out=dst, in_=src)
+        def abs_gelu(j):
+            nc.scalar.activation(out=tiles["gelu", j][:], in_=tiles["gelu", j][:], func=ACT.Abs)
 
-        def tquant(kind, q, c):
-            codes, planes = (dy_codes, dy_planes) if kind == "dy" else (w2_codes, w2_planes)
-            sl = slice(512 * q, 512 * q + 512)
-            nc.vector.quantize_mx(out=codes[:, c, sl].bitcast(X4), scales=planes[:, c, sl], in_=GRP[kind, q, c][:])
-            give("grp%s%d%d" % (kind, q, c))
-            if c == 1:
-                give("raw%s%d" % (kind, q))
-
-        def xw(g, ts=(0, 1, 2, 3), eng="V"):
-            if g not in XW:
-                XW[g] = take("big", "xw%d" % g, [P, 4, D], BF16)
-            for t in ts:
-                src = XB[g][:, t, :].bitcast(FP8)
-                if eng == "V":
-                    nc.vector.tensor_scalar(out=XW[g][:, t, :], in0=src, scalar1=xs[:, g, t:t + 1], scalar2=None, op0=ALU.mult)
-                else:
-                    nc.scalar.activation(out=XW[g][:, t, :], in_=src, func=ACT.Copy, scale=xs[:, g, t:t + 1])
-                if t == 3:
-                    give("xb%d" % g)
-
-        def xi(g, h):
-            if h == 0:
-                XI[g] = take("big", "xi%d" % g, [P, 4096], BF16)
-            nc.vector.tensor_copy(out=XI[g][:, 2048 * h:2048 * h + 2048].rearrange("p (c i t) -> p c t i", i=4, t=4), in_=XW[g][:, :, 512 * h:512 * h + 512].rearrange("p t (c i) -> p c t i", i=4))
-            if h == 1:
-                give("xw%d" % g)
-
-        def xq(g):
-            nc.vector.quantize_mx(out=x_codes[:, g, :].bitcast(X4), scales=x_planes[:, g, :], in_=XI[g][:])
-            give("xi%d" % g)
-
-        def v1(j):
-            nc.vector.tensor_tensor(out=G[j][:], in0=G[j][:], in1=R[j][:], op=ALU.mult)
-            give("r%d" % j)
-
-        def v2(j):
-            nc.vector.scalar_tensor_tensor(out=E[j][:], in0=a_unit(j), scalar=INV_SQRT_2PI, in1=E[j][:], op0=ALU.mult, op1=ALU.mult)
-            done_a(j)
-
-        def v3(j):
-            nc.vector.tensor_tensor(out=G[j][:], in0=G[j][:], in1=E[j][:], op=ALU.add)
-            give("e%d" % j)
-
-        def s1(j, g):
-            bank = ps.tile([P, 4, P], F32, name="dh", bufs=DB)
-            S1[j, g] = bank
-            for t in range(4):
-                for c in range(2):
-                    col = 512 * g + 128 * t
-                    nc.tensor.matmul_mx(
-                        out=bank[:, t, :], lhsT=dy_codes[:, c, col:col + 128].bitcast(X4), lhsT_scale=dy_planes[:, c, col:col + 128],
-                        rhs=w2_codes[:, c, 128 * j:128 * j + 128].bitcast(X4), rhs_scale=w2_planes[:, c, 128 * j:128 * j + 128],
-                        start=(c == 0), stop=(c == 1))
-
-        def v4(j, g):
-            if g == 0:
-                DQ[j] = take("small", "daq%d" % j, [P, 2048], BF16)
-            nc.vector.tensor_tensor(
-                out=DQ[j][:, 512 * g:512 * g + 512].rearrange("p (c i t) -> p c t i", i=4, t=4),
-                in0=S1[j, g][:].rearrange("p t (c i) -> p c t i", i=4), in1=G[j][:, 4 * g:4 * g + 4, :].rearrange("p t (c i) -> p c t i", i=4), op=ALU.mult)
-            if g == 3:
-                give("g%d" % j)
-
-        def q(j):
-            DC[j] = keep.tile([P, 512], U32, name="dac", bufs=2, align_bytes=64)
-            DPL[j] = keep.tile([P, 512], U8, name="dap", bufs=2, align_bytes=64)
-            nc.vector.quantize_mx(out=DC[j][:].bitcast(X4), scales=DPL[j][:], in_=DQ[j][:])
-            give("daq%d" % j)
-
-        def s2(j, hb):
-            bank = ps.tile([P, 4, P], F32, name="gp", bufs=2)
-            S2[j, hb] = bank
-            for k in range(4):
-                i = 4 * hb + k
-                for g in range(NG):
-                    nc.tensor.matmul_mx(
-                        out=bank[:, k, :], lhsT=x_codes[:, g, 128 * i:128 * i + 128].bitcast(X4), lhsT_scale=x_planes[:, g, 128 * i:128 * i + 128],
-                        rhs=DC[j][:, 128 * g:128 * g + 128].bitcast(X4), rhs_scale=DPL[j][:, 128 * g:128 * g + 128],
-                        start=(g == 0), stop=(g == NG - 1))
-
-        def fc(j):
-            return slice(128 * (j % 2), 128 * (j % 2) + 128)
-
-        def sq(j, hb):
-            if hb == 0:
-                SQ[j] = take("small", "sq%d" % j, [P, 8, P], F32)
-            nc.scalar.activation(out=SQ[j][:, 4 * hb:4 * hb + 4, :], in_=S2[j, hb][:], func=ACT.Square, scale=math.sqrt(0.4 / 0.6 / T))
-
-        def p_(j, hb):
+        def gaussian_term(j):
+            e = tiles["gauss", j]
             nc.vector.scalar_tensor_tensor(
-                out=r_sb[:, 4 * hb:4 * hb + 4, 128 * j:128 * j + 128], in0=MV["m", j // 2][:, 4 * hb:4 * hb + 4, fc(j)], scalar=1.5 * math.sqrt(T),
-                in1=S2[j, hb][:], op0=ALU.mult, op1=ALU.add)
-            MV_USE.append(j // 2)
-            if MV_USE.count(j // 2) == 6:
-                give("mv%d" % (j // 2))
+                out=e[:], in0=a_unit(j), scalar=INV_SQRT_2PI, in1=e[:], op0=ALU.mult, op1=ALU.mult
+            )
+            used_a(j)
 
-        def vn(j):
-            nc.vector.tensor_tensor(out=SQ[j][:], in0=MV["v", j // 2][:, :, fc(j)], in1=SQ[j][:], op=ALU.add)
-            MV_USE.append(j // 2)
-            if MV_USE.count(j // 2) == 6:
-                give("mv%d" % (j // 2))
+        def normal_cdf(j):
+            nc.vector.tensor_tensor(
+                out=tiles["gelu", j][:], in0=tiles["gelu", j][:], in1=tiles["root", j][:], op=ALU.mult
+            )
+            give_unit("root", j)
 
-        def rs(j):
-            nc.scalar.activation(out=SQ[j][:], in_=SQ[j][:], func=ACT.Abs_reciprocal_sqrt, scale=0.6 * T / 0.16)
+        def gelu_slope(j):
+            nc.vector.tensor_tensor(
+                out=tiles["gelu", j][:], in0=tiles["gelu", j][:], in1=tiles["gauss", j][:], op=ALU.add
+            )
+            give_unit("gauss", j)
 
-        def mm(j):
-            rj = r_sb[:, :, 128 * j:128 * j + 128]
-            nc.vector.tensor_tensor(out=rj, in0=rj, in1=SQ[j][:], op=ALU.mult)
-            if j < NU - 1:
-                give("sq%d" % j)
 
-        def rr(j):
-            nc.vector.scalar_tensor_tensor(out=SQ[j][:], in0=w1_sb[:, :, 128 * j:128 * j + 128], scalar=0.1, in1=r_sb[:, :, 128 * j:128 * j + 128], op0=ALU.mult, op1=ALU.add)
+        def multiply_dh(j, g):
+            bank = psum.tile([P, PACK, P], F32, name="dh", bufs=DH_BANKS)
+            tiles["dh", j, g] = bank
+            for t in range(PACK):
+                tokens = slice(PASS * g + P * t, PASS * g + P * (t + 1))
+                columns = slice(P * j, P * (j + 1))
+                for c in range(WIDTH_PASSES):
+                    nc.tensor.matmul_mx(
+                        out=bank[:, t, :],
+                        lhsT=dy_codes[:, c, tokens].bitcast(FP8X4),
+                        lhsT_scale=dy_mx_scales[:, c, tokens],
+                        rhs=w2_codes[:, c, columns].bitcast(FP8X4),
+                        rhs_scale=w2_mx_scales[:, c, columns],
+                        start=(c == 0),
+                        stop=(c == WIDTH_PASSES - 1),
+                    )
 
-        def rn(j):
-            nc.scalar.activation(out=SQ[j][:], in_=SQ[j][:], func=ACT.Square, accum_out=stat[:, 0:1])
+        def da_product(j, g):
+            if g == 0:
+                tiles["da", j] = take("small", "da%d" % j, [P, TOKEN_PASSES * PACK * P], BF16)
+            order = "p t (c i) -> p c t i"
+            nc.vector.tensor_tensor(
+                out=tiles["da", j][:, PASS * g : PASS * (g + 1)].rearrange("p (c i t) -> p c t i", i=4, t=PACK),
+                in0=tiles["dh", j, g][:].rearrange(order, i=4),
+                in1=tiles["gelu", j][:, PACK * g : PACK * (g + 1), :].rearrange(order, i=4),
+                op=ALU.mult,
+            )
+            if g == TOKEN_PASSES - 1:
+                give("gelu%d" % j)
 
-        def wf(j, eng):
-            WF[j] = take("small", "wf%d" % j, [P, 8, P], F32)
-            src = w1_sb[:, :, 128 * j:128 * j + 128]
-            if eng == "S":
-                nc.scalar.activation(out=WF[j][:], in_=src, func=ACT.Copy, scale=0.2)
-            else:
-                nc.vector.tensor_scalar(out=WF[j][:], in0=src, scalar1=0.2, scalar2=None, op0=ALU.mult)
+        def quantise_da(j):
+            tiles["da_codes", j] = keep.tile([P, PASS], U32, name="da_codes", bufs=2, align_bytes=64)
+            tiles["da_scales", j] = keep.tile([P, PASS], U8, name="da_scales", bufs=2, align_bytes=64)
+            nc.vector.quantize_mx(
+                out=tiles["da_codes", j][:].bitcast(FP8X4), scales=tiles["da_scales", j][:], in_=tiles["da", j][:]
+            )
+            give("da%d" % j)
 
-        def nn(j):
+
+        def multiply_g(j, h):
+            bank = psum.tile([P, 4, P], F32, name="g", bufs=G_BANKS)
+            tiles["g", j, h] = bank
+            for k in range(4):
+                rows = slice(P * (4 * h + k), P * (4 * h + k + 1))
+                for g in range(TOKEN_PASSES):
+                    columns = slice(P * g, P * (g + 1))
+                    nc.tensor.matmul_mx(
+                        out=bank[:, k, :],
+                        lhsT=x_codes[:, g, rows].bitcast(FP8X4),
+                        lhsT_scale=x_mx_scales[:, g, rows],
+                        rhs=tiles["da_codes", j][:, columns].bitcast(FP8X4),
+                        rhs_scale=tiles["da_scales", j][:, columns],
+                        start=(g == 0),
+                        stop=(g == TOKEN_PASSES - 1),
+                    )
+
+        def half_of(h):
+            return slice(0, ROW_TILES) if h is None else slice(4 * h, 4 * h + 4)
+
+        def columns_of(j):
+            return slice(P * j, P * (j + 1))
+
+        def moment_of(which, j, h):
+            return tiles[which, j // 2][:, half_of(h), P * (j % 2) : P * (j % 2) + P]
+
+        def square_g(j, h):
+            if h == 0:
+                tiles["v_new", j] = take("small", "v_new%d" % j, [P, ROW_TILES, P], F32)
+            nc.scalar.activation(
+                out=tiles["v_new", j][:, half_of(h), :],
+                in_=tiles["g", j, h][:],
+                func=ACT.Square,
+                scale=math.sqrt(0.4 / 0.6 / TOKENS),
+            )
+
+        def first_moment(j, h):
+            nc.vector.scalar_tensor_tensor(
+                out=tiles["rho"][:, half_of(h), columns_of(j)],
+                in0=moment_of("m", j, h),
+                scalar=0.6 / 0.4 * math.sqrt(TOKENS),
+                in1=tiles["g", j, h][:],
+                op0=ALU.mult,
+                op1=ALU.add,
+            )
+
+        def second_moment(j, h=None):
+            part = tiles["v_new", j][:, half_of(h), :]
+            nc.vector.tensor_tensor(out=part, in0=moment_of("v", j, h), in1=part, op=ALU.add)
+
+        def rsqrt_v(j, h=None):
+            part = tiles["v_new", j][:, half_of(h), :]
+            nc.scalar.activation(
+                out=part, in_=part, func=ACT.Abs_reciprocal_sqrt, scale=0.6 * TOKENS / (0.4 * 0.4)
+            )
+
+        def make_rho(j, h=None):
+            part = tiles["rho"][:, half_of(h), columns_of(j)]
+            nc.vector.tensor_tensor(out=part, in0=part, in1=tiles["v_new", j][:, half_of(h), :], op=ALU.mult)
+            if h != 0:
+                if j != LAST:
+                    give("v_new%d" % j)
+                if j % 2 == 1:
+                    give("moments%d" % (j // 2))
+
+        def widen_w1(j):
+            tiles["w1_f32", j] = take("small", "w1_f32%d" % j, [P, ROW_TILES, P], F32)
+            nc.scalar.activation(
+                out=tiles["w1_f32", j][:], in_=w1_tile[:, :, columns_of(j)], func=ACT.Copy, scale=0.2
+            )
+
+
+        def multiply_rho(j, h=None):
             if j == 0:
-                NB.append(ps.tile([P, P], F32, name="nrm", bufs=1))
-            for i in range(8):
-                rho = r_sb[:, i, 128 * j:128 * j + 128]
-                nc.tensor.matmul(out=NB[0][:], lhsT=rho, rhs=rho, start=(j == 0 and i == 0), stop=False)
-                nc.tensor.matmul(out=NB[0][:], lhsT=rho, rhs=WF[j][:, i, :], start=False, stop=(j == NU - 2 and i == 7))
-            give("wf%d" % j)
+                tiles["norm"] = psum.tile([P, P], F32, name="norm", bufs=1)
+            for i in range(ROW_TILES)[half_of(h)]:
+                block = tiles["rho"][:, i, columns_of(j)]
+                first, last = (j, i) == (0, 0), (j, i) == (LAST - 1, ROW_TILES - 1)
+                nc.tensor.matmul(out=tiles["norm"][:], lhsT=block, rhs=block, start=first, stop=False)
+                nc.tensor.matmul(
+                    out=tiles["norm"][:], lhsT=block, rhs=tiles["w1_f32", j][:, i, :], start=False, stop=last
+                )
+            if h != 0:
+                give("w1_f32%d" % j)
 
-        WN = {}
+        def last_r(h):
+            nc.vector.scalar_tensor_tensor(
+                out=tiles["v_new", LAST][:, half_of(h), :],
+                in0=w1_tile[:, half_of(h), columns_of(LAST)],
+                scalar=0.1,
+                in1=tiles["rho"][:, half_of(h), columns_of(LAST)],
+                op0=ALU.mult,
+                op1=ALU.add,
+            )
 
-        def wn():
-            WN["bank"] = ps.tile([P, 2, P], F32, name="tp", bufs=TB)
-            for s, units in enumerate((range(NU - 1), range(NU - 1, NU))):
-                blocks = [(i, j) for j in units for i in range(8)]
+        def last_r_square(h):
+            part = tiles["v_new", LAST][:, half_of(h), :]
+            nc.scalar.activation(out=part, in_=part, func=ACT.Square, accum_out=sums[:, h : h + 1])
+
+        def multiply_w1():
+            tiles["w1_gram"] = psum.tile([P, 2, P], F32, name="turned", bufs=TURN_BANKS)
+            for s, units in enumerate((range(LAST), range(LAST, UNITS))):
+                blocks = [(i, j) for j in units for i in range(ROW_TILES)]
                 for n, (i, j) in enumerate(blocks):
-                    blk = w1_sb[:, i, 128 * j:128 * j + 128]
-                    nc.tensor.matmul(out=WN["bank"][:, s, :], lhsT=blk, rhs=blk, start=(n == 0), stop=(n == len(blocks) - 1))
+                    block = w1_tile[:, i, columns_of(j)]
+                    nc.tensor.matmul(
+                        out=tiles["w1_gram"][:, s, :],
+                        lhsT=block,
+                        rhs=block,
+                        start=(n == 0),
+                        stop=(n == len(blocks) - 1),
+                    )
 
-        def wt():
-            tr = keep.tile([P, 2, P], F32, name="tr")
+        def w1_diagonal():
             for s in range(2):
-                nc.vector.tensor_tensor(out=tr[:, s, :], in0=WN["bank"][:, s, :], in1=ident[:], op=ALU.mult)
-            nc.vector.tensor_reduce(out=stat[:, 18:20], in_=tr[:], axis=AX.X, op=ALU.add)
+                nc.vector.tensor_tensor(
+                    out=diagonal[:, s, :], in0=tiles["w1_gram"][:, s, :], in1=identity[:], op=ALU.mult
+                )
+            nc.vector.tensor_reduce(out=sums[:, 3:5], in_=diagonal[:], axis=AXIS.X, op=ALU.add)
 
-        def wt2():
-            WN["sum"] = ps.tile([P, 2], F32, name="tp", bufs=TB)
-            nc.tensor.matmul(out=WN["sum"][:], lhsT=ones[:], rhs=stat[:, 18:20], start=True, stop=True)
+        def w1_total():
+            total = psum.tile([P, 2], F32, name="turned", bufs=TURN_BANKS)
+            nc.tensor.matmul(out=total[:], lhsT=ones[:], rhs=sums[:, 3:5], start=True, stop=True)
+            tiles["w1_total"] = total
 
-        def wv():
-            nc.vector.tensor_reduce(out=wtot[:, 0:1], in_=WN["sum"][:], axis=AX.X, op=ALU.add)
+        def w1_square():
+            nc.vector.tensor_reduce(out=w1_norm[:, 0:1], in_=tiles["w1_total"][:], axis=AXIS.X, op=ALU.add)
 
-        def wr():
-            nc.scalar.activation(out=wtot[:, 1:2], in_=wtot[:, 0:1], func=ACT.Abs_reciprocal_sqrt, bias=1e-30)
+        def w1_rsqrt():
+            nc.scalar.activation(
+                out=w1_norm[:, 1:2], in_=w1_norm[:, 0:1], func=ACT.Abs_reciprocal_sqrt, bias=1e-30
+            )
 
-        def wx():
-            nc.vector.tensor_tensor(out=wtot[:, 2:3], in0=wtot[:, 0:1], in1=wtot[:, 1:2], op=ALU.mult)
+        def w1_root():
+            nc.vector.tensor_scalar(
+                out=w1_norm[:, 2:3],
+                in0=w1_norm[:, 0:1],
+                scalar1=w1_norm[:, 1:2],
+                scalar2=-0.5,
+                op0=ALU.mult,
+                op1=ALU.mult,
+            )
+            nc.vector.tensor_scalar(
+                out=w1_norm[:, 3:4], in0=w1_norm[:, 2:3], scalar1=0.1, scalar2=None, op0=ALU.mult
+            )
 
-        def trace_rho():
-            tr = keep.tile([P, P], F32, name="tr2")
-            nc.vector.tensor_tensor(out=tr[:], in0=NB[0][:], in1=ident[:], op=ALU.mult)
-            nc.vector.tensor_reduce(out=stat[:, 1:2], in_=tr[:], axis=AX.X, op=ALU.add)
-            nc.vector.scalar_tensor_tensor(out=stat[:, 1:2], in0=stat[:, 18:19], scalar=0.01, in1=stat[:, 1:2], op0=ALU.mult, op1=ALU.add)
+        def rho_diagonal():
+            nc.vector.tensor_tensor(
+                out=diagonal[:, 0, :], in0=tiles["norm"][:], in1=identity[:], op=ALU.mult
+            )
+            nc.vector.tensor_reduce(out=sums[:, 2:3], in_=diagonal[:, 0, :], axis=AXIS.X, op=ALU.add)
+            nc.vector.scalar_tensor_tensor(
+                out=sums[:, 2:3], in0=sums[:, 3:4], scalar=0.01, in1=sums[:, 2:3], op0=ALU.mult, op1=ALU.add
+            )
 
-        def tail():
-            nc.vector.tensor_tensor(out=stat[:, 17:18], in0=stat[:, 0:1], in1=stat[:, 1:2], op=ALU.add)
-            b2 = ps.tile([P, 1], F32, name="tp", bufs=TB)
-            nc.tensor.matmul(out=b2[:], lhsT=ones[:], rhs=stat[:, 17:18], start=True, stop=True)
-            nc.scalar.activation(out=wtot[:, 3:4], in_=b2[:], func=ACT.Abs_reciprocal_sqrt)
-            nc.vector.tensor_scalar(out=wtot[:, 4:5], in0=wtot[:, 3:4], scalar1=wtot[:, 2:3], scalar2=-0.5, op0=ALU.mult, op1=ALU.mult)
-            nc.vector.tensor_scalar(out=wtot[:, 5:6], in0=wtot[:, 4:5], scalar1=0.1, scalar2=1.0, op0=ALU.mult, op1=ALU.add)
-            o = out.rearrange("(i p) f -> i p f", p=P)
-            for i in range(8):
-                wa = take("big", "wa%d" % i, [P, F], F32)
-                nc.scalar.activation(out=wa[:], in_=w1_sb[:, i, :], func=ACT.Copy, scale=wtot[:, 5:6])
-                nc.vector.scalar_tensor_tensor(out=r_sb[:, i, :], in0=r_sb[:, i, :], scalar=wtot[:, 4:5], in1=wa[:], op0=ALU.mult, op1=ALU.add)
-                give("wa%d" % i)
-                nc.sync.dma_start(out=o[i], in_=r_sb[:, i, :])
+        def update():
+            total = psum.tile([P, 1], F32, name="turned", bufs=TURN_BANKS)
+            for n, k in enumerate((2, 0, 1)):
+                nc.tensor.matmul(
+                    out=total[:], lhsT=ones[:], rhs=sums[:, k : k + 1], start=(n == 0), stop=(n == 2)
+                )
+            give("v_new%d" % LAST)
+            nc.scalar.activation(out=trust[:, 0:1], in_=total[:], func=ACT.Abs_reciprocal_sqrt)
+            nc.vector.tensor_tensor(out=trust[:, 1:2], in0=trust[:, 0:1], in1=w1_norm[:, 2:3], op=ALU.mult)
+            nc.scalar.activation(
+                out=trust[:, 2:3], in_=trust[:, 0:1], func=ACT.Copy, scale=w1_norm[:, 3:4], bias=1.0
+            )
+            rows = out.rearrange("(i p) f -> i p f", p=P)
+            middle = HIDDEN // 2
+            for i in range(ROW_TILES):
+                w1_part = take("big", "w1_part%d" % i, [P, HIDDEN], F32)
+                for c in (slice(0, middle), slice(middle, HIDDEN)) if i == 0 else (slice(0, HIDDEN),):
+                    if i == 0 and c.start == 0:
+                        nc.vector.tensor_scalar(
+                            out=w1_part[:, c],
+                            in0=w1_tile[:, i, c],
+                            scalar1=trust[:, 2:3],
+                            scalar2=None,
+                            op0=ALU.mult,
+                        )
+                    else:
+                        nc.scalar.activation(
+                            out=w1_part[:, c], in_=w1_tile[:, i, c], func=ACT.Copy, scale=trust[:, 2:3]
+                        )
+                    nc.vector.scalar_tensor_tensor(
+                        out=tiles["rho"][:, i, c],
+                        in0=tiles["rho"][:, i, c],
+                        scalar=trust[:, 1:2],
+                        in1=w1_part[:, c],
+                        op0=ALU.mult,
+                        op1=ALU.add,
+                    )
+                    nc.sync.dma_start(out=rows[i][:, c], in_=tiles["rho"][:, i, c])
+                give("w1_part%d" % i)
+
+
+        turns = [(index, c, b) for index in (4, 0, 1, 2, 3, 5) for c in range(WIDTH_PASSES) for b in range(2)]
+        dhs = [(j, g) for j in range(UNITS) for g in range(TOKEN_PASSES)]
+        gs = [(j, h) for j in range(UNITS) for h in range(2)]
+        count = {"turn": 0, "dh": 0, "g": 0}
+
+        def issued(name, *index):
+            return ".".join([name] + [str(n) for n in index]) in done
+
+        def bank_free(kind, n, banks, *readers):
+            return n < banks or all(issued(reader, *kind[n - banks]) for reader in readers)
+
+        def tensor_step():
+            n = count["turn"]
+            if n < len(turns) and issued("rows", turns[n][0]) and bank_free(turns, n, TURN_BANKS, "copied"):
+                turn(*turns[n])
+                count["turn"] += 1
+                return True
+            n = count["dh"]
+            if n < len(dhs):
+                j, g = dhs[n]
+                ready = issued("tq", g, 1) and issued("tq", TOKEN_PASSES + j // (UNITS // 2), 1)
+                if ready and bank_free(dhs, n, DH_BANKS, "da"):
+                    multiply_dh(j, g)
+                    count["dh"] += 1
+                    return True
+            n = count["g"]
+            if n < len(gs):
+                ready = issued("qd", gs[n][0]) and all(issued("xq", g) for g in range(TOKEN_PASSES))
+                if ready and bank_free(gs, n, G_BANKS, "sq", "m1"):
+                    multiply_g(*gs[n])
+                    count["g"] += 1
+                    return True
+            return False
+
+        steps = {
+            "a": load_a, "x": load_x, "dy": load_dy, "w2": load_w2, "mv": load_moments, "w1": load_w1,
+            "xw": widen_x, "xi": interleave_x, "xq": quantise_x,
+            "cs": copy_on_scalar, "cv": copy_on_vector, "tq": quantise_turned,
+            "z": square_a, "r": rsqrt_z, "e": exp_z, "ge": gelu_a, "ab": abs_gelu,
+            "ph": gaussian_term, "cdf": normal_cdf, "gp": gelu_slope, "da": da_product, "qd": quantise_da,
+            "sq": square_g, "m1": first_moment, "m2": second_moment, "rs": rsqrt_v, "rho": make_rho,
+            "wf": widen_w1, "lr": last_r, "lq": last_r_square,
+            "wm": multiply_w1, "nm": multiply_rho, "wt": w1_total, "wd": w1_diagonal, "ws": w1_square, "wr": w1_rsqrt, "wn": w1_root, "rd": rho_diagonal,
+        }
+
         nc.vector.memset(ones[:], 1.0)
-        nc.scalar.activation(out=wtot[:, 7:8], in_=ones[:, 0:1], func=ACT.Abs_reciprocal_sqrt)
-        make_identity(nc, ident[:])
-        nc.sync.dma_start(out=xs[:], in_=x_scale.rearrange("(g p t) o -> p g (t o)", g=NG, t=4))
-        load_x(0)
-        load_a(0, 0)
-        load_a(0, 1)
-        z(0, True, [0, 1])
-        load_a(0, 2)
-        load_a(0, 3)
-        z(1, True)
-        xw(0, (0, 1, 2, 3), "V")
-        xi(0, 0)
-        xi(0, 1)
-        z(0, True, [2, 3])
-        load_raw("w2", 0)
-        tp("w2", 0, 0, 0)
-        xq(0)
-        load_raw("dy", 0)
-        tcopy("w2", 0, 0, 0, "V")
-        load_x(1)
-        rr_(1, True)
-        tp("w2", 0, 0, 1)
-        tp("w2", 0, 1, 0)
-        tcopy("w2", 0, 0, 1, "V")
-        tcopy("w2", 0, 1, 0, "V")
-        load_raw("dy", 1)
-        rr_(0, True)
-        tp("w2", 0, 1, 1)
-        tquant("w2", 0, 0)
-        tcopy("w2", 0, 1, 1, "S")
-        tp("dy", 0, 0, 0)
-        xw(1, (0, 1, 2, 3), "V")
-        gl(0)
-        load_raw("dy", 2)
-        tp("dy", 0, 0, 1)
-        tcopy("dy", 0, 0, 0, "V")
-        xi(1, 0)
-        tcopy("dy", 0, 0, 1, "S")
-        tquant("w2", 0, 1)
-        tp("dy", 0, 1, 0)
-        tp("dy", 0, 1, 1)
-        tcopy("dy", 0, 1, 0, "S")
-        xi(1, 1)
-        load_x(2)
-        tp("dy", 1, 0, 0)
-        xw(2, (0, 1, 2, 3), "V")
-        tcopy("dy", 0, 1, 1, "V")
-        xq(1)
-        tp("dy", 1, 0, 1)
-        ab(0)
-        tcopy("dy", 1, 0, 0, "S")
-        load_a(1)
-        tp("dy", 1, 1, 0)
-        tquant("dy", 0, 0)
-        xi(2, 0)
-        v1(0)
-        gl(1)
-        load_raw("dy", 3)
-        gl(3)
-        tcopy("dy", 1, 0, 1, "V")
-        tcopy("dy", 1, 1, 0, "S")
-        tp("dy", 1, 1, 1)
-        gl(2)
-        xi(2, 1)
-        tquant("dy", 0, 1)
-        load_x(3)
-        tp("dy", 2, 0, 0)
-        tcopy("dy", 1, 1, 1, "S")
-        tcopy("dy", 2, 0, 0, "S")
-        load_raw("w2", 1)
-        xw(3, (0, 1, 2, 3), "V")
-        z(3, False)
-        tquant("dy", 1, 0)
-        xi(3, 0)
-        tquant("dy", 1, 1)
-        tp("dy", 2, 0, 1)
-        tp("dy", 2, 1, 0)
-        tcopy("dy", 2, 0, 1, "S")
-        tcopy("dy", 2, 1, 0, "S")
-        tp("dy", 2, 1, 1)
-        tcopy("dy", 2, 1, 1, "V")
-        tp("dy", 3, 0, 0)
-        e(0, True)
-        tp("dy", 3, 0, 1)
-        s1(0, 0)
-        tcopy("dy", 3, 0, 0, "S")
-        xi(3, 1)
-        e(3, False)
-        xq(2)
-        tquant("dy", 2, 0)
-        load_a(2)
-        xq(3)
-        tp("dy", 3, 1, 0)
-        tcopy("dy", 3, 0, 1, "V")
-        tcopy("dy", 3, 1, 0, "S")
-        e(1, True)
-        tp("dy", 3, 1, 1)
-        tcopy("dy", 3, 1, 1, "S")
-        v2(0)
-        s1(0, 1)
-        tquant("dy", 2, 1)
-        ab(1)
-        tp("w2", 1, 0, 0)
-        s1(0, 2)
-        tcopy("w2", 1, 0, 0, "S")
-        v3(0)
-        load_w1()
-        tquant("dy", 3, 0)
-        v4(0, 0)
-        z(2, False)
-        tquant("dy", 3, 1)
-        s1(0, 3)
-        tp("w2", 1, 0, 1)
-        v4(0, 1)
-        tcopy("w2", 1, 0, 1, "S")
-        v1(1)
-        v2(1)
-        s1(1, 0)
-        tp("w2", 1, 1, 0)
-        tp("w2", 1, 1, 1)
-        e(2, False)
-        tcopy("w2", 1, 1, 0, "S")
-        v2(3)
-        v4(0, 2)
-        v3(1)
-        load_mv(0)
-        v4(0, 3)
-        ab(2)
-        s1(1, 1)
-        v4(1, 0)
-        q(0)
-        v4(1, 1)
-        rr_(2, False)
-        ab(3)
-        s1(1, 2)
-        s1(1, 3)
-        s2(0, 0)
-        load_a(3)
-        tquant("w2", 1, 0)
-        tcopy("w2", 1, 1, 1, "S")
-        rr_(3, False)
-        v4(1, 2)
-        sq(0, 0)
-        s2(0, 1)
-        v1(2)
-        v2(2)
-        z(4, True)
-        wn()
-        v4(1, 3)
-        tquant("w2", 1, 1)
-        v3(2)
-        r_sb = mem.tile([P, 8, F], F32, name="r_sb", bufs=1, offset=8192 * NBIG)
-        p_(0, 0)
-        s1(2, 0)
-        s1(2, 1)
-        sq(0, 1)
-        q(1)
-        s1(2, 2)
-        v4(2, 0)
-        s1(2, 3)
-        vn(0)
-        rr_(4, True)
-        v1(3)
-        v4(2, 1)
-        v3(3)
-        v4(2, 2)
-        wt()
-        z(5, True)
-        s2(1, 0)
-        p_(0, 1)
-        s1(3, 0)
-        load_mv(1)
-        e(4, True)
-        v4(3, 0)
-        v4(2, 3)
-        wf(0, "V")
-        s2(1, 1)
-        sq(1, 0)
-        s1(3, 1)
-        gl(4)
-        s1(3, 2)
-        gl(5)
-        sq(1, 1)
-        p_(1, 0)
-        v4(3, 1)
-        s1(3, 3)
-        p_(1, 1)
-        v4(3, 2)
-        q(2)
-        ab(4)
-        s1(4, 0)
-        s1(4, 1)
-        v4(3, 3)
-        gl(6)
-        v2(4)
-        s2(2, 0)
-        sq(2, 0)
-        v1(4)
-        rs(0)
-        wt2()
-        q(3)
-        s2(2, 1)
-        vn(1)
-        sq(2, 1)
-        s1(4, 2)
-        p_(2, 0)
-        rr_(5, True)
-        mm(0)
-        v3(4)
-        vn(2)
-        v4(4, 0)
-        rs(1)
-        s2(3, 0)
-        e(5, True)
-        p_(2, 1)
-        ab(5)
-        mm(1)
-        nn(0)
-        wf(1, "V")
-        s1(4, 3)
-        z(7, False)
-        v4(4, 1)
-        s2(3, 1)
-        v1(5)
-        v4(4, 2)
-        sq(3, 0)
-        p_(3, 0)
-        v2(5)
-        wv()
-        v3(5)
-        s1(5, 0)
-        nn(1)
-        z(6, False)
-        sq(3, 1)
-        s1(5, 1)
-        v4(4, 3)
-        e(6, False)
-        ab(6)
-        load_mv(2)
-        v4(5, 0)
-        q(4)
-        s2(4, 0)
-        e(7, False)
-        p_(3, 1)
-        rr_(6, False)
-        v4(5, 1)
-        wr()
-        rs(2)
-        v2(6)
-        s1(5, 2)
-        v4(5, 2)
-        s1(5, 3)
-        s1(6, 0)
-        vn(3)
-        wf(2, "S")
-        sq(4, 0)
-        v4(5, 3)
-        v1(6)
-        rr_(7, False)
-        s1(6, 1)
-        s2(4, 1)
-        mm(2)
-        v3(6)
-        q(5)
-        sq(4, 1)
-        v4(6, 0)
-        vn(4)
-        s1(6, 2)
-        nn(2)
-        v4(6, 1)
-        rs(3)
-        wf(3, "S")
-        s1(6, 3)
-        p_(4, 0)
-        mm(3)
-        gl(7)
-        v4(6, 2)
-        s1(7, 0)
-        p_(4, 1)
-        s2(5, 0)
-        load_mv(3)
-        v4(6, 3)
-        v2(7)
-        sq(5, 0)
-        s1(7, 1)
-        s2(5, 1)
-        ab(7)
-        p_(5, 0)
-        s1(7, 2)
-        nn(3)
-        q(6)
-        sq(5, 1)
-        rs(4)
-        v1(7)
-        p_(5, 1)
-        s2(6, 0)
-        sq(6, 0)
-        wf(4, "S")
-        s2(6, 1)
-        v3(7)
-        wx()
-        sq(6, 1)
-        v4(7, 0)
-        mm(4)
-        p_(6, 0)
-        s1(7, 3)
-        v4(7, 1)
-        vn(5)
-        v4(7, 2)
-        rs(5)
-        wf(5, "S")
-        v4(7, 3)
-        nn(4)
-        q(7)
-        mm(5)
-        p_(6, 1)
-        s2(7, 0)
-        sq(7, 0)
-        s2(7, 1)
-        vn(6)
-        nn(5)
-        sq(7, 1)
-        p_(7, 0)
-        wf(6, "V")
-        p_(7, 1)
-        vn(7)
-        rs(6)
-        mm(6)
-        nn(6)
-        rs(7)
-        mm(7)
-        rr(7)
-        rn(7)
-        trace_rho()
-        tail()
+        nc.scalar.activation(out=trust[:, 0:1], in_=ones[:, 0:1], func=ACT.Abs_reciprocal_sqrt)
+        make_identity(nc, identity[:])
+        nc.scalar.dma_start(out=x_scales[:], in_=x_scale.rearrange("(g p t) o -> p g (t o)", g=TOKEN_PASSES, t=PACK))
+
+        for step in ORDER:
+            parts = step.split(".")
+            name, index = parts[0], parts[1:]
+            while tensor_step():
+                pass
+            if name == "m1" and "rho" not in tiles:
+                tiles["rho"] = mem.tile([P, ROW_TILES, HIDDEN], F32, name="rho", bufs=1, offset=BIG_BYTES * BIG)
+            steps[name](*[int(n) for n in index])
+            done.add(step)
+            if name in ("dy", "w2"):
+                done.add("rows.%d" % (int(index[0]) + (TOKEN_PASSES if name == "w2" else 0)))
+        update()

@@ -36,24 +36,25 @@ BIG_BYTES, SMALL_BYTES = 8192, 4096
 TURN_BANKS, DH_BANKS, G_BANKS = 2, 3, 2
 
 ORDER = """
-x.0.0 a.0.0 xw.0.0 x.0.1 a.0.1 a.0.2 a.0.3 w2.0 xw.0.1 xi.0.0 xi.0.1 xq.0 z.0.0 dy.0 z.0.1
-x.1 z.1 dy.1 cv.4.0.0 cv.4.0.1 tq.4.0 cv.4.1.0 r.0 xw.1 cv.0.0.0 xi.1.0 r.1 cs.4.1.1 dy.2 cv.0.0.1
-xi.1.1 cv.0.1.0 x.2 tq.4.1 ge.1 ge.0 cs.1.0.0 cv.0.1.1 ab.0 xw.2 cs.1.0.1 cv.1.1.0 tq.0.0 cdf.0 xq.1
-ab.1 cs.1.1.1 tq.1.0 a.1 cs.2.0.0 ge.2 tq.0.1 cv.2.0.1 e.0 dy.3 xi.2.0 x.3 cv.2.1.0 xw.3 z.2
-tq.2.0 cs.3.0.0 xi.3.0 ab.2 cv.2.1.1 tq.1.1 z.3 ph.0 xi.2.1 cs.3.0.1 e.1 xi.3.1 cv.3.1.0 gp.0 w2.1
-cs.3.1.1 tq.3.0 e.3 a.2 da.0.0 tq.2.1 tq.3.1 cv.5.0.0 da.0.1 e.2 xq.2 cdf.1 ph.1 r.3 da.0.2
-cv.5.0.1 r.2 z.5 ph.2 gp.1 cs.5.1.0 da.0.3 r.5 z.4 tq.5.0 xq.3 da.1.0 e.4 cdf.2 e.5
-ge.3 da.1.1 gp.2 da.1.2 w1 qd.0 cv.5.1.1 da.2.0 da.1.3 mv.0 da.2.1 sq.0.0 ph.3 ge.5 qd.1
-tq.5.1 wm sq.0.1 da.2.2 ph.4 m2.0 ab.3 m1.0.0 da.2.3 m1.0.1 ph.5 ge.4 a.3 cdf.3 rs.0
-mv.1 sq.1.0 rho.0 wf.0 nm.0 gp.3 sq.1.1 m1.1.0 m2.1 da.3.0 r.4 qd.2 da.3.1 m1.1.1 ab.4
-da.3.2 ab.5 cdf.4 rs.1 sq.2.0 wf.1 da.3.3 rho.1 z.6 m1.2.0 nm.1 sq.2.1 gp.4 mv.2 r.6
-m2.2 da.4.0 qd.3 wf.2 rs.2 e.6 da.4.1 sq.3.0 m1.2.1 cdf.5 da.4.2 rho.2 ge.6 gp.5 mv.3
-nm.2 ph.6 da.4.3 da.5.0 sq.3.1 m2.3 m1.3.0 qd.4 ge.7 rs.3 da.5.1 sq.4.0 ab.6 m1.3.1 da.5.2
-wd sq.4.1 wt da.5.3 rho.3 wf.3 m1.4.0 qd.5 z.7 sq.5.0 cdf.6 m2.4 r.7 rs.4 nm.3
-gp.6 m1.5.0 da.6.0 ab.7 wf.4 m1.4.1 da.6.1 rho.4 da.6.2 sq.5.1 nm.4 cdf.7 e.7 da.6.3 wf.6
-m1.5.1 wf.5 qd.6 m2.5 rs.5 ph.7 sq.6.0 gp.7 sq.6.1 ws da.7.0 rho.5 nm.5 m2.6.1 m2.6.0
-rs.6.1 m1.6.0 da.7.1 rs.6.0 da.7.2 m1.6.1 da.7.3 qd.7 wr sq.7.0 rho.6.0 rho.6.1 m2.7.0 m1.7.0 sq.7.1
-rs.7.0 m2.7.1 wn rs.7.1 rho.7.0 nm.6.0 m1.7.1 rho.7.1 nm.6.1 lr.0 lr.1 rd lq.1 lq.0
+x.0.0 xw.0.0 a.0.0 x.0.1 xw.0.1 a.0.1 xi.0.0 xi.0.1 a.0.2 xq.0 a.0.3 w2.0 z.0.0 dy.0 z.1
+cv.4.0.0 z.0.1 cv.4.0.1 x.1 r.1 dy.1 tq.4.0 cs.4.1.0 xw.1 cv.4.1.1 cv.0.0.0 xi.1.0 r.0 dy.2 cv.0.0.1
+x.2 tq.4.1 a.1 ge.0 ge.1 cv.0.1.0 tq.0.0 cv.0.1.1 xw.2 xi.1.1 cs.1.0.0 dy.3 xi.2.0 ab.0 xq.1
+cs.1.1.0 xi.2.1 cv.1.0.1 cdf.0 ge.2 cv.1.1.1 x.3 cv.2.0.0 e.0 xq.2 tq.1.0 ab.1 tq.0.1 ph.0 cs.2.1.0
+cs.2.0.1 e.1 cv.2.1.1 tq.2.0 cs.3.0.0 w2.1 gp.0 z.3 ab.2 cs.3.1.0 cv.3.0.1 xw.3 tq.3.0 a.2 z.2
+da.0.0 cs.3.1.1 cs.5.0.0 cdf.1 tq.2.1 cv.5.0.1 tq.1.1 xi.3.0 ph.1 xi.3.1 e.3 cs.5.1.0 w1 tq.3.1 da.0.1
+z.4 gp.1 e.2 da.0.2 da.1.0 da.0.3 e.4 cv.5.1.1 qd.0 da.1.1 mv.0 xq.3 wm r.2 tq.5.0
+ph.2 wf.0 ge.5 sq.0.0 tq.5.1 da.1.2 ge.3 cdf.2 da.1.3 sq.0.1 ab.3 ge.4 gp.2 m2.0 da.2.0
+rs.0 m1.0.0 qd.1 da.2.1 sq.1.0 m1.0.1 r.3 ph.3 da.2.2 rho.0 nm.0.0 da.2.3 sq.1.1 a.3 wf.1
+cdf.3 nm.0.1 r.4 qd.2 m1.1.0 gp.3 m2.1 z.5 wf.2 da.3.0 m1.1.1 rs.1 ab.4 da.3.1 rho.1
+sq.2.0 z.6 nm.1.0 ph.4 da.3.2 cdf.4 nm.1.1 mv.1 m1.2.0 sq.2.1 da.3.3 gp.4 r.5 mv.2 qd.3
+m2.2 da.4.0 r.6 m1.2.1 ab.5 da.4.1 rs.2 rho.2 sq.3.0 nm.2.0 da.4.2 e.5 cdf.5 nm.2.1 m1.3.0
+sq.3.1 da.4.3 e.6 ph.5 qd.4 ge.7 ge.6 gp.5 da.5.0 m1.3.1 da.5.1 m2.3 da.5.2 wd wt
+sq.4.0 rs.3 da.5.3 m1.4.0 mv.3 qd.5 wf.3 rho.3 sq.4.1 ws nm.3.0 ab.6 z.7 ph.6 nm.3.1
+m2.4 m1.4.1 cdf.6 rs.4 sq.5.0 wr rho.4 wf.4 gp.6 r.7 sq.5.1 nm.4.0 da.6.0 nm.4.1 da.6.1
+m2.5 ab.7 da.6.2 e.7 rs.5 m1.5.1 cdf.7 wf.5 da.6.3 m1.5.0 qd.6 ph.7 sq.6.0 rho.5 nm.5.0
+gp.7 wf.6 da.7.0 m1.6.0 nm.5.1 da.7.1 da.7.2 sq.6.1 da.7.3 qd.7 m2.6.0 m1.6.1 rs.6.0 wn m2.6.1
+rs.6.1 sq.7.0 rho.6.0 m2.7.0 sq.7.1 rho.6.1 m2.7.1 rs.7.0 nm.6.0 m1.7.0 m1.7.1 rho.7.0 rs.7.1 rho.7.1 nm.6.1
+lr.0 lr.1 rd lq.0 lq.1
 """.split()
 
 
@@ -395,7 +396,7 @@ def tile_lambmlpbackwardstep_kernel(tc, x_bytes, x_scale, a, dy, w2, w1, m, v, o
 
 
         def multiply_rho(j, h=None):
-            if j == 0:
+            if "norm" not in tiles:
                 tiles["norm"] = psum.tile([P, P], F32, name="norm", bufs=1)
             for i in range(ROW_TILES)[half_of(h)]:
                 block = tiles["rho"][:, i, columns_of(j)]

import math
from contextlib import ExitStack

import concourse.mybir as mybir
from concourse.masks import make_identity

TOKENS, WIDTH, HIDDEN = 2048, 1024, 1024

F32 = mybir.dt.float32
BF16 = mybir.dt.bfloat16
U32 = mybir.dt.uint32
U8 = mybir.dt.uint8
FP8 = mybir.dt.float8_e4m3fn
FP8X4 = mybir.dt.float8_e4m3fn_x4
ACT = mybir.ActivationFunctionType
ALU = mybir.AluOpType
AXIS = mybir.AxisListType

P = 128
PACK = 4
PASS = P * PACK
TOKEN_PASSES = TOKENS // PASS
WIDTH_PASSES = WIDTH // PASS
ROW_TILES = WIDTH // P
UNITS = HIDDEN // P
LAST = UNITS - 1

DELTA = 2.0**-60
INV_SQRT_2PI = 1.0 / math.sqrt(2.0 * math.pi)

FLOPS = 2 * 2 * TOKENS * WIDTH * HIDDEN

BIG, RAW, SMALL = 14, 4, 5
BIG_BYTES, SMALL_BYTES = 8192, 4096

TURN_BANKS, DH_BANKS, G_BANKS = 2, 3, 2

ORDER = """
x.0.0 xw.0.0 a.0.0 x.0.1 xw.0.1 a.0.1 xi.0.0 xi.0.1 a.0.2 xq.0 a.0.3 w2.0 z.0.0 dy.0 z.1
cv.4.0.0 z.0.1 cv.4.0.1 x.1 r.1 dy.1 tq.4.0 cs.4.1.0 xw.1 cv.4.1.1 cv.0.0.0 xi.1.0 r.0 dy.2 cv.0.0.1
x.2 tq.4.1 a.1 ge.0 ge.1 cv.0.1.0 tq.0.0 cv.0.1.1 xw.2 xi.1.1 cs.1.0.0 dy.3 xi.2.0 ab.0 xq.1
cs.1.1.0 xi.2.1 cv.1.0.1 cdf.0 ge.2 cv.1.1.1 x.3 cv.2.0.0 e.0 xq.2 tq.1.0 ab.1 tq.0.1 ph.0 cs.2.1.0
cs.2.0.1 e.1 cv.2.1.1 tq.2.0 cs.3.0.0 w2.1 gp.0 z.3 ab.2 cs.3.1.0 cv.3.0.1 xw.3 tq.3.0 a.2 z.2
da.0.0 cs.3.1.1 cs.5.0.0 cdf.1 tq.2.1 cv.5.0.1 tq.1.1 xi.3.0 ph.1 xi.3.1 e.3 cs.5.1.0 w1 tq.3.1 da.0.1
z.4 gp.1 e.2 da.0.2 da.1.0 da.0.3 e.4 cv.5.1.1 qd.0 da.1.1 mv.0 xq.3 wm r.2 tq.5.0
ph.2 wf.0 ge.5 sq.0.0 tq.5.1 da.1.2 ge.3 cdf.2 da.1.3 sq.0.1 ab.3 ge.4 gp.2 m2.0 da.2.0
rs.0 m1.0.0 qd.1 da.2.1 sq.1.0 m1.0.1 r.3 ph.3 da.2.2 rho.0 nm.0.0 da.2.3 sq.1.1 a.3 wf.1
cdf.3 nm.0.1 r.4 qd.2 m1.1.0 gp.3 m2.1 z.5 wf.2 da.3.0 m1.1.1 rs.1 ab.4 da.3.1 rho.1
sq.2.0 z.6 nm.1.0 ph.4 da.3.2 cdf.4 nm.1.1 mv.1 m1.2.0 sq.2.1 da.3.3 gp.4 r.5 mv.2 qd.3
m2.2 da.4.0 r.6 m1.2.1 ab.5 da.4.1 rs.2 rho.2 sq.3.0 nm.2.0 da.4.2 e.5 cdf.5 nm.2.1 m1.3.0
sq.3.1 da.4.3 e.6 ph.5 qd.4 ge.7 ge.6 gp.5 da.5.0 m1.3.1 da.5.1 m2.3 da.5.2 wd wt
sq.4.0 rs.3 da.5.3 m1.4.0 mv.3 qd.5 wf.3 rho.3 sq.4.1 ws nm.3.0 ab.6 z.7 ph.6 nm.3.1
m2.4 m1.4.1 cdf.6 rs.4 sq.5.0 wr rho.4 wf.4 gp.6 r.7 sq.5.1 nm.4.0 da.6.0 nm.4.1 da.6.1
m2.5 ab.7 da.6.2 e.7 rs.5 m1.5.1 cdf.7 wf.5 da.6.3 m1.5.0 qd.6 ph.7 sq.6.0 rho.5 nm.5.0
gp.7 wf.6 da.7.0 m1.6.0 nm.5.1 da.7.1 da.7.2 sq.6.1 da.7.3 qd.7 m2.6.0 m1.6.1 rs.6.0 wn m2.6.1
rs.6.1 sq.7.0 rho.6.0 m2.7.0 sq.7.1 rho.6.1 m2.7.1 rs.7.0 nm.6.0 m1.7.0 m1.7.1 rho.7.0 rs.7.1 rho.7.1 nm.6.1
lr.0 lr.1 rd lq.0 lq.1
""".split()


def tile_lambmlpbackwardstep_kernel(tc, x_bytes, x_scale, a, dy, w2, w1, m, v, out):
    nc = tc.nc
    with ExitStack() as ctx:
        keep = ctx.enter_context(tc.tile_pool(name="keep", bufs=1))
        mem = ctx.enter_context(tc.tile_pool(name="mem", bufs=1))
        psum = ctx.enter_context(tc.psum_pool(name="psum", bufs=2))
        ctx.enter_context(tc.manual_schedule())

        identity = keep.tile([P, P], F32, name="identity")
        ones = keep.tile([P, P], F32, name="ones")
        x_scales = keep.tile([P, TOKEN_PASSES, PACK], F32, name="x_scales")
        x_codes = keep.tile([P, TOKEN_PASSES, WIDTH], U32, name="x_codes", align_bytes=64)
        x_mx_scales = keep.tile([P, TOKEN_PASSES, WIDTH], U8, name="x_mx_scales", align_bytes=64)
        dy_codes = keep.tile([P, WIDTH_PASSES, TOKENS], U32, name="dy_codes", align_bytes=64)
        dy_mx_scales = keep.tile([P, WIDTH_PASSES, TOKENS], U8, name="dy_mx_scales", align_bytes=64)
        w2_codes = keep.tile([P, WIDTH_PASSES, HIDDEN], U32, name="w2_codes", align_bytes=64)
        w2_mx_scales = keep.tile([P, WIDTH_PASSES, HIDDEN], U8, name="w2_mx_scales", align_bytes=64)
        w1_tile = keep.tile([P, ROW_TILES, HIDDEN], BF16, name="w1_tile")
        diagonal = keep.tile([P, 2, P], F32, name="diagonal")
        sums = keep.tile([P, 8], F32, name="sums")
        w1_norm = keep.tile([P, 8], F32, name="w1_norm")
        trust = keep.tile([P, 8], F32, name="trust")

        free = {
            "big": [BIG_BYTES * s for s in range(BIG)],
            "raw": [BIG_BYTES * (BIG + s) for s in range(RAW)],
            "small": [BIG_BYTES * (BIG + RAW) + SMALL_BYTES * s for s in range(SMALL)],
        }
        owner = {}

        def take(kind, name, shape, dtype):
            owner[name] = (kind, free[kind].pop(0))
            return mem.tile(shape, dtype, name=name, bufs=1, offset=owner[name][1], align_bytes=64)

        def give(name):
            kind, offset = owner.pop(name)
            free[kind].append(offset)

        done = set()
        tiles = {}


        def load_a(pair, g=None):
            if ("a", pair) not in tiles:
                tiles["a", pair] = take("big", "a%d" % pair, [P, TOKEN_PASSES * PACK, 2 * P], BF16)
            source = a.rearrange("(g p t) f -> p g t f", g=TOKEN_PASSES, t=PACK)
            for q in range(TOKEN_PASSES) if g is None else (g,):
                nc.sync.dma_start(
                    out=tiles["a", pair][:, PACK * q : PACK * q + PACK, :],
                    in_=source[:, q, :, 2 * P * pair : 2 * P * (pair + 1)],
                )

        def load_x(g, half=None):
            if ("x", g) not in tiles:
                tiles["x", g] = take("small", "x_raw%d" % g, [P, PACK, WIDTH], U8)
            ts = slice(0, PACK) if half is None else slice(2 * half, 2 * half + 2)
            source = x_bytes.rearrange("(g p t) d -> g p t d", g=TOKEN_PASSES, t=PACK)
            nc.sync.dma_start(out=tiles["x", g][:, ts, :], in_=source[g][:, ts, :])

        def load_dy(g):
            tiles["rows", g] = take("raw", "dy_rows%d" % g, [P, PACK, WIDTH], BF16)
            source = dy.rearrange("(g p t) k -> g p t k", g=TOKEN_PASSES, t=PACK)
            nc.sync.dma_start(out=tiles["rows", g][:], in_=source[g])

        def load_w2(half):
            index = TOKEN_PASSES + half
            tiles["rows", index] = take("raw", "w2_rows%d" % half, [P, 4, WIDTH], BF16)
            source = w2.rearrange("(h b p) k -> h p b k", h=2, b=4)
            nc.sync.dma_start(out=tiles["rows", index][:], in_=source[half])

        def load_moments(pair):
            both = take("big", "moments%d" % pair, [P, 2 * ROW_TILES, 2 * P], BF16)
            for n, source in enumerate((m, v)):
                tiles["mv"[n], pair] = both[:, ROW_TILES * n : ROW_TILES * (n + 1), :]
                nc.sync.dma_start(
                    out=tiles["mv"[n], pair],
                    in_=source.rearrange("(i p) f -> p i f", p=P)[:, :, 2 * P * pair : 2 * P * (pair + 1)],
                )

        def load_w1():
            nc.sync.dma_start(out=w1_tile[:], in_=w1.rearrange("(i p) f -> p i f", p=P))


        def widen_x(g, half=None):
            if half in (None, 0):
                tiles["pairs", g] = take("big", "x_pairs%d" % g, [P, 2, WIDTH, 2], BF16)
            for t in range(PACK) if half is None else (2 * half, 2 * half + 1):
                nc.vector.tensor_scalar(
                    out=tiles["pairs", g][:, t // 2, :, t % 2],
                    in0=tiles["x", g][:, t, :].bitcast(FP8),
                    scalar1=x_scales[:, g, t : t + 1],
                    scalar2=None,
                    op0=ALU.mult,
                )
            if half in (None, 1):
                give("x_raw%d" % g)

        def interleave_x(g, half):
            if half == 0:
                tiles["x_bf16", g] = take("big", "x_bf16%d" % g, [P, PACK * WIDTH], BF16)
            n = WIDTH // 2
            words = tiles["pairs", g][:].rearrange("p u n e -> p (u n e)").bitcast(F32)
            nc.vector.tensor_copy(
                out=tiles["x_bf16", g][:, PACK * n * half : PACK * n * (half + 1)]
                .bitcast(F32)
                .rearrange("p (n u) -> p n u", u=2),
                in_=words.rearrange("p (u n) -> p n u", u=2)[:, n * half : n * (half + 1), :],
            )
            if half == 1:
                give("x_pairs%d" % g)

        def quantise_x(g):
            nc.vector.quantize_mx(
                out=x_codes[:, g, :].bitcast(FP8X4), scales=x_mx_scales[:, g, :], in_=tiles["x_bf16", g][:]
            )
            give("x_bf16%d" % g)


        def turn(index, c, b):
            bank = psum.tile([P, 2, 2, P], F32, name="turned", bufs=TURN_BANKS)
            tiles["turned", index, c, b] = bank
            for k in range(2):
                words = tiles["rows", index][:, 2 * b + k, :].bitcast(F32)
                for u in range(2):
                    nc.tensor.transpose(
                        out=bank[:, k, u, :],
                        in_=words[:, PASS // 2 * c + u : PASS // 2 * (c + 1) : 2],
                        identity=identity[:],
                    )

        def copy_turned(index, c, b, on_scalar):
            name = "turned%d%d" % (index, c)
            if b == 0:
                tiles["grouped", index, c] = take("small", name, [P, PACK * PASS], BF16)
            out_words = tiles["grouped", index, c][:].bitcast(F32)[:, PASS * b : PASS * (b + 1)]
            out_words = out_words.rearrange("p (k r u) -> p k r u", k=2, u=2)
            in_words = tiles["turned", index, c, b][:].rearrange("p k u r -> p k r u")
            if on_scalar:
                nc.scalar.copy(out=out_words, in_=in_words)
            else:
                nc.vector.tensor_copy(out=out_words, in_=in_words)
            done.add("copied.%d.%d.%d" % (index, c, b))

        def copy_on_scalar(index, c, b):
            copy_turned(index, c, b, True)

        def copy_on_vector(index, c, b):
            copy_turned(index, c, b, False)

        def quantise_turned(index, c):
            if index < TOKEN_PASSES:
                codes, scales, first = dy_codes, dy_mx_scales, PASS * index
            else:
                codes, scales, first = w2_codes, w2_mx_scales, PASS * (index - TOKEN_PASSES)
            columns = slice(first, first + PASS)
            nc.vector.quantize_mx(
                out=codes[:, c, columns].bitcast(FP8X4),
                scales=scales[:, c, columns],
                in_=tiles["grouped", index, c][:],
            )
            give("turned%d%d" % (index, c))
            if c == WIDTH_PASSES - 1:
                give(("dy_rows%d" % index) if index < TOKEN_PASSES else ("w2_rows%d" % (index - TOKEN_PASSES)))


        uses_of_a = []

        def a_unit(j):
            return tiles["a", j // 2][:, :, P * (j % 2) : P * (j % 2) + P]

        def used_a(j):
            uses_of_a.append(j // 2)
            if uses_of_a.count(j // 2) == 4:
                give("a%d" % (j // 2))

        def unit_tile(what, j):
            tiles[what, j] = take("big", "%s%d" % (what, j), [P, TOKEN_PASSES * PACK, P], F32)
            return tiles[what, j]

        def square_a(j, half=None):
            z = unit_tile("z", j) if half in (None, 0) else tiles["z", j]
            part = slice(0, 16) if half is None else slice(8 * half, 8 * half + 8)
            nc.scalar.activation(out=z[:, part, :], in_=a_unit(j)[:, part, :], func=ACT.Square)

        def rsqrt_z(j):
            z = tiles["z", j]
            tiles["root", j] = z if ("gauss", j) in tiles else unit_tile("root", j)
            nc.scalar.activation(
                out=tiles["root", j][:], in_=z[:], func=ACT.Abs_reciprocal_sqrt, bias=DELTA * DELTA
            )

        def exp_z(j):
            z = tiles["z", j]
            tiles["gauss", j] = z if ("root", j) in tiles else unit_tile("gauss", j)
            nc.scalar.activation(out=tiles["gauss", j][:], in_=z[:], func=ACT.Exp, scale=-0.5)

        def give_unit(what, j):
            give("%s%d" % ("z" if tiles[what, j] is tiles["z", j] else what, j))

        def gelu_a(j):
            nc.scalar.activation(out=unit_tile("gelu", j)[:], in_=a_unit(j), func=ACT.Gelu, bias=DELTA)
            used_a(j)

        def abs_gelu(j):
            nc.scalar.activation(out=tiles["gelu", j][:], in_=tiles["gelu", j][:], func=ACT.Abs)

        def gaussian_term(j):
            e = tiles["gauss", j]
            nc.vector.scalar_tensor_tensor(
                out=e[:], in0=a_unit(j), scalar=INV_SQRT_2PI, in1=e[:], op0=ALU.mult, op1=ALU.mult
            )
            used_a(j)

        def normal_cdf(j):
            nc.vector.tensor_tensor(
                out=tiles["gelu", j][:], in0=tiles["gelu", j][:], in1=tiles["root", j][:], op=ALU.mult
            )
            give_unit("root", j)

        def gelu_slope(j):
            nc.vector.tensor_tensor(
                out=tiles["gelu", j][:], in0=tiles["gelu", j][:], in1=tiles["gauss", j][:], op=ALU.add
            )
            give_unit("gauss", j)


        def multiply_dh(j, g):
            bank = psum.tile([P, PACK, P], F32, name="dh", bufs=DH_BANKS)
            tiles["dh", j, g] = bank
            for t in range(PACK):
                tokens = slice(PASS * g + P * t, PASS * g + P * (t + 1))
                columns = slice(P * j, P * (j + 1))
                for c in range(WIDTH_PASSES):
                    nc.tensor.matmul_mx(
                        out=bank[:, t, :],
                        lhsT=dy_codes[:, c, tokens].bitcast(FP8X4),
                        lhsT_scale=dy_mx_scales[:, c, tokens],
                        rhs=w2_codes[:, c, columns].bitcast(FP8X4),
                        rhs_scale=w2_mx_scales[:, c, columns],
                        start=(c == 0),
                        stop=(c == WIDTH_PASSES - 1),
                    )

        def da_product(j, g):
            if g == 0:
                tiles["da", j] = take("small", "da%d" % j, [P, TOKEN_PASSES * PACK * P], BF16)
            order = "p t (c i) -> p c t i"
            nc.vector.tensor_tensor(
                out=tiles["da", j][:, PASS * g : PASS * (g + 1)].rearrange("p (c i t) -> p c t i", i=4, t=PACK),
                in0=tiles["dh", j, g][:].rearrange(order, i=4),
                in1=tiles["gelu", j][:, PACK * g : PACK * (g + 1), :].rearrange(order, i=4),
                op=ALU.mult,
            )
            if g == TOKEN_PASSES - 1:
                give("gelu%d" % j)

        def quantise_da(j):
            tiles["da_codes", j] = keep.tile([P, PASS], U32, name="da_codes", bufs=2, align_bytes=64)
            tiles["da_scales", j] = keep.tile([P, PASS], U8, name="da_scales", bufs=2, align_bytes=64)
            nc.vector.quantize_mx(
                out=tiles["da_codes", j][:].bitcast(FP8X4), scales=tiles["da_scales", j][:], in_=tiles["da", j][:]
            )
            give("da%d" % j)


        def multiply_g(j, h):
            bank = psum.tile([P, 4, P], F32, name="g", bufs=G_BANKS)
            tiles["g", j, h] = bank
            for k in range(4):
                rows = slice(P * (4 * h + k), P * (4 * h + k + 1))
                for g in range(TOKEN_PASSES):
                    columns = slice(P * g, P * (g + 1))
                    nc.tensor.matmul_mx(
                        out=bank[:, k, :],
                        lhsT=x_codes[:, g, rows].bitcast(FP8X4),
                        lhsT_scale=x_mx_scales[:, g, rows],
                        rhs=tiles["da_codes", j][:, columns].bitcast(FP8X4),
                        rhs_scale=tiles["da_scales", j][:, columns],
                        start=(g == 0),
                        stop=(g == TOKEN_PASSES - 1),
                    )

        def half_of(h):
            return slice(0, ROW_TILES) if h is None else slice(4 * h, 4 * h + 4)

        def columns_of(j):
            return slice(P * j, P * (j + 1))

        def moment_of(which, j, h):
            return tiles[which, j // 2][:, half_of(h), P * (j % 2) : P * (j % 2) + P]

        def square_g(j, h):
            if h == 0:
                tiles["v_new", j] = take("small", "v_new%d" % j, [P, ROW_TILES, P], F32)
            nc.scalar.activation(
                out=tiles["v_new", j][:, half_of(h), :],
                in_=tiles["g", j, h][:],
                func=ACT.Square,
                scale=math.sqrt(0.4 / 0.6 / TOKENS),
            )

        def first_moment(j, h):
            nc.vector.scalar_tensor_tensor(
                out=tiles["rho"][:, half_of(h), columns_of(j)],
                in0=moment_of("m", j, h),
                scalar=0.6 / 0.4 * math.sqrt(TOKENS),
                in1=tiles["g", j, h][:],
                op0=ALU.mult,
                op1=ALU.add,
            )

        def second_moment(j, h=None):
            part = tiles["v_new", j][:, half_of(h), :]
            nc.vector.tensor_tensor(out=part, in0=moment_of("v", j, h), in1=part, op=ALU.add)

        def rsqrt_v(j, h=None):
            part = tiles["v_new", j][:, half_of(h), :]
            nc.scalar.activation(
                out=part, in_=part, func=ACT.Abs_reciprocal_sqrt, scale=0.6 * TOKENS / (0.4 * 0.4)
            )

        def make_rho(j, h=None):
            part = tiles["rho"][:, half_of(h), columns_of(j)]
            nc.vector.tensor_tensor(out=part, in0=part, in1=tiles["v_new", j][:, half_of(h), :], op=ALU.mult)
            if h != 0:
                if j != LAST:
                    give("v_new%d" % j)
                if j % 2 == 1:
                    give("moments%d" % (j // 2))

        def widen_w1(j):
            tiles["w1_f32", j] = take("small", "w1_f32%d" % j, [P, ROW_TILES, P], F32)
            nc.scalar.activation(
                out=tiles["w1_f32", j][:], in_=w1_tile[:, :, columns_of(j)], func=ACT.Copy, scale=0.2
            )


        def multiply_rho(j, h=None):
            if "norm" not in tiles:
                tiles["norm"] = psum.tile([P, P], F32, name="norm", bufs=1)
            for i in range(ROW_TILES)[half_of(h)]:
                block = tiles["rho"][:, i, columns_of(j)]
                first, last = (j, i) == (0, 0), (j, i) == (LAST - 1, ROW_TILES - 1)
                nc.tensor.matmul(out=tiles["norm"][:], lhsT=block, rhs=block, start=first, stop=False)
                nc.tensor.matmul(
                    out=tiles["norm"][:], lhsT=block, rhs=tiles["w1_f32", j][:, i, :], start=False, stop=last
                )
            if h != 0:
                give("w1_f32%d" % j)

        def last_r(h):
            nc.vector.scalar_tensor_tensor(
                out=tiles["v_new", LAST][:, half_of(h), :],
                in0=w1_tile[:, half_of(h), columns_of(LAST)],
                scalar=0.1,
                in1=tiles["rho"][:, half_of(h), columns_of(LAST)],
                op0=ALU.mult,
                op1=ALU.add,
            )

        def last_r_square(h):
            part = tiles["v_new", LAST][:, half_of(h), :]
            nc.scalar.activation(out=part, in_=part, func=ACT.Square, accum_out=sums[:, h : h + 1])

        def multiply_w1():
            tiles["w1_gram"] = psum.tile([P, 2, P], F32, name="turned", bufs=TURN_BANKS)
            for s, units in enumerate((range(LAST), range(LAST, UNITS))):
                blocks = [(i, j) for j in units for i in range(ROW_TILES)]
                for n, (i, j) in enumerate(blocks):
                    block = w1_tile[:, i, columns_of(j)]
                    nc.tensor.matmul(
                        out=tiles["w1_gram"][:, s, :],
                        lhsT=block,
                        rhs=block,
                        start=(n == 0),
                        stop=(n == len(blocks) - 1),
                    )

        def w1_diagonal():
            for s in range(2):
                nc.vector.tensor_tensor(
                    out=diagonal[:, s, :], in0=tiles["w1_gram"][:, s, :], in1=identity[:], op=ALU.mult
                )
            nc.vector.tensor_reduce(out=sums[:, 3:5], in_=diagonal[:], axis=AXIS.X, op=ALU.add)

        def w1_total():
            total = psum.tile([P, 2], F32, name="turned", bufs=TURN_BANKS)
            nc.tensor.matmul(out=total[:], lhsT=ones[:], rhs=sums[:, 3:5], start=True, stop=True)
            tiles["w1_total"] = total

        def w1_square():
            nc.vector.tensor_reduce(out=w1_norm[:, 0:1], in_=tiles["w1_total"][:], axis=AXIS.X, op=ALU.add)

        def w1_rsqrt():
            nc.scalar.activation(
                out=w1_norm[:, 1:2], in_=w1_norm[:, 0:1], func=ACT.Abs_reciprocal_sqrt, bias=1e-30
            )

        def w1_root():
            nc.vector.tensor_scalar(
                out=w1_norm[:, 2:3],
                in0=w1_norm[:, 0:1],
                scalar1=w1_norm[:, 1:2],
                scalar2=-0.5,
                op0=ALU.mult,
                op1=ALU.mult,
            )
            nc.vector.tensor_scalar(
                out=w1_norm[:, 3:4], in0=w1_norm[:, 2:3], scalar1=0.1, scalar2=None, op0=ALU.mult
            )

        def rho_diagonal():
            nc.vector.tensor_tensor(
                out=diagonal[:, 0, :], in0=tiles["norm"][:], in1=identity[:], op=ALU.mult
            )
            nc.vector.tensor_reduce(out=sums[:, 2:3], in_=diagonal[:, 0, :], axis=AXIS.X, op=ALU.add)
            nc.vector.scalar_tensor_tensor(
                out=sums[:, 2:3], in0=sums[:, 3:4], scalar=0.01, in1=sums[:, 2:3], op0=ALU.mult, op1=ALU.add
            )

        def update():
            total = psum.tile([P, 1], F32, name="turned", bufs=TURN_BANKS)
            for n, k in enumerate((2, 0, 1)):
                nc.tensor.matmul(
                    out=total[:], lhsT=ones[:], rhs=sums[:, k : k + 1], start=(n == 0), stop=(n == 2)
                )
            give("v_new%d" % LAST)
            nc.scalar.activation(out=trust[:, 0:1], in_=total[:], func=ACT.Abs_reciprocal_sqrt)
            nc.vector.tensor_tensor(out=trust[:, 1:2], in0=trust[:, 0:1], in1=w1_norm[:, 2:3], op=ALU.mult)
            nc.scalar.activation(
                out=trust[:, 2:3], in_=trust[:, 0:1], func=ACT.Copy, scale=w1_norm[:, 3:4], bias=1.0
            )
            rows = out.rearrange("(i p) f -> i p f", p=P)
            middle = HIDDEN // 2
            for i in range(ROW_TILES):
                w1_part = take("big", "w1_part%d" % i, [P, HIDDEN], F32)
                for c in (slice(0, middle), slice(middle, HIDDEN)) if i == 0 else (slice(0, HIDDEN),):
                    if i == 0 and c.start == 0:
                        nc.vector.tensor_scalar(
                            out=w1_part[:, c],
                            in0=w1_tile[:, i, c],
                            scalar1=trust[:, 2:3],
                            scalar2=None,
                            op0=ALU.mult,
                        )
                    else:
                        nc.scalar.activation(
                            out=w1_part[:, c], in_=w1_tile[:, i, c], func=ACT.Copy, scale=trust[:, 2:3]
                        )
                    nc.vector.scalar_tensor_tensor(
                        out=tiles["rho"][:, i, c],
                        in0=tiles["rho"][:, i, c],
                        scalar=trust[:, 1:2],
                        in1=w1_part[:, c],
                        op0=ALU.mult,
                        op1=ALU.add,
                    )
                    nc.sync.dma_start(out=rows[i][:, c], in_=tiles["rho"][:, i, c])
                give("w1_part%d" % i)


        turns = [(index, c, b) for index in (4, 0, 1, 2, 3, 5) for c in range(WIDTH_PASSES) for b in range(2)]
        dhs = [(j, g) for j in range(UNITS) for g in range(TOKEN_PASSES)]
        gs = [(j, h) for j in range(UNITS) for h in range(2)]
        count = {"turn": 0, "dh": 0, "g": 0}

        def issued(name, *index):
            return ".".join([name] + [str(n) for n in index]) in done

        def bank_free(kind, n, banks, *readers):
            return n < banks or all(issued(reader, *kind[n - banks]) for reader in readers)

        def tensor_step():
            n = count["turn"]
            if n < len(turns) and issued("rows", turns[n][0]) and bank_free(turns, n, TURN_BANKS, "copied"):
                turn(*turns[n])
                count["turn"] += 1
                return True
            n = count["dh"]
            if n < len(dhs):
                j, g = dhs[n]
                ready = issued("tq", g, 1) and issued("tq", TOKEN_PASSES + j // (UNITS // 2), 1)
                if ready and bank_free(dhs, n, DH_BANKS, "da"):
                    multiply_dh(j, g)
                    count["dh"] += 1
                    return True
            n = count["g"]
            if n < len(gs):
                ready = issued("qd", gs[n][0]) and all(issued("xq", g) for g in range(TOKEN_PASSES))
                if ready and bank_free(gs, n, G_BANKS, "sq", "m1"):
                    multiply_g(*gs[n])
                    count["g"] += 1
                    return True
            return False

        steps = {
            "a": load_a, "x": load_x, "dy": load_dy, "w2": load_w2, "mv": load_moments, "w1": load_w1,
            "xw": widen_x, "xi": interleave_x, "xq": quantise_x,
            "cs": copy_on_scalar, "cv": copy_on_vector, "tq": quantise_turned,
            "z": square_a, "r": rsqrt_z, "e": exp_z, "ge": gelu_a, "ab": abs_gelu,
            "ph": gaussian_term, "cdf": normal_cdf, "gp": gelu_slope, "da": da_product, "qd": quantise_da,
            "sq": square_g, "m1": first_moment, "m2": second_moment, "rs": rsqrt_v, "rho": make_rho,
            "wf": widen_w1, "lr": last_r, "lq": last_r_square,
            "wm": multiply_w1, "nm": multiply_rho, "wt": w1_total, "wd": w1_diagonal, "ws": w1_square, "wr": w1_rsqrt, "wn": w1_root, "rd": rho_diagonal,
        }

        nc.vector.memset(ones[:], 1.0)
        nc.scalar.activation(out=trust[:, 0:1], in_=ones[:, 0:1], func=ACT.Abs_reciprocal_sqrt)
        make_identity(nc, identity[:])
        nc.scalar.dma_start(out=x_scales[:], in_=x_scale.rearrange("(g p t) o -> p g (t o)", g=TOKEN_PASSES, t=PACK))

        for step in ORDER:
            parts = step.split(".")
            name, index = parts[0], parts[1:]
            while tensor_step():
                pass
            if name == "m1" and "rho" not in tiles:
                tiles["rho"] = mem.tile([P, ROW_TILES, HIDDEN], F32, name="rho", bufs=1, offset=BIG_BYTES * BIG)
            steps[name](*[int(n) for n in index])
            done.add(step)
            if name in ("dy", "w2"):
                done.add("rows.%d" % (int(index[0]) + (TOKEN_PASSES if name == "w2" else 0)))
        update()
